import numpy as np
import ml_dtypes


def mxq(x, axis, fmt="e4m3"):
    dtype, down = {"e4m3": (ml_dtypes.float8_e4m3fn, 7), "e5m2": (ml_dtypes.float8_e5m2, 14)}[fmt]
    v = np.moveaxis(np.asarray(x, np.float32).astype(ml_dtypes.bfloat16).astype(np.float64), axis, -1)
    blocks = v.reshape(v.shape[:-1] + (-1, 32))
    amax = np.abs(blocks).max(-1, keepdims=True)
    byte = np.maximum(np.where(amax > 0, np.frexp(amax)[1] - 1 + 127, 0) - down, 1)
    scale = np.exp2(byte - 127.0)
    codes = (blocks / scale).astype(np.float32).astype(dtype).astype(np.float64)
    return np.moveaxis((codes * scale).reshape(v.shape), -1, axis)


WIDE = False


def mx_kscale(k):
    if not WIDE:
        return np.ones(k)
    levels = np.array([10, -10, 5, -5, 0])
    if k % 512:
        return np.exp2(np.random.permutation(np.resize(levels, k // 32))).repeat(32)
    a = np.empty((k // 512, 16))
    for p in range(k // 512):
        a[p, :8] = np.random.permutation(np.resize(levels, 8))
        for g in range(8):
            far = levels[np.abs(levels - a[p, g]) >= 10]
            a[p, g + 8] = far[np.random.randint(len(far))]
    return np.exp2(a.ravel()).repeat(32)


def f64(x):
    return np.asarray(x).astype(np.float64)


def striped(idx):
    return np.tile(idx.reshape(-1, 16).T, (8, 1)).astype(np.uint16)


def unstriped(offs):
    return offs[:16].T.reshape(-1).astype(np.int64)


E2M1 = np.array([0.0, 0.5, 1.0, 1.5, 2.0, 3.0, 4.0, 6.0, -0.0, -0.5, -1.0, -1.5, -2.0, -3.0, -4.0, -6.0])


def pack_weight(w, fmt):
    k, n = w.shape
    w = f64(np.asarray(w, np.float32).astype(ml_dtypes.bfloat16)).reshape(k // 32, 32, n)
    amax = np.abs(w).max(1)
    if fmt == "e4m3":
        byte = np.frexp(amax)[1] - 1 + 127 - 7
    else:
        mant, ex = np.frexp(amax / 6.0)
        byte = np.where(mant > 0.5, ex, ex - 1) + 127
    byte = np.clip(np.where(amax > 0, byte, 1), 1, 254)
    scaled = (w * np.exp2(127.0 - byte)[:, None, :]).reshape(k, n).astype(np.float32)
    by_word = np.ascontiguousarray(scaled.reshape(k // 512, 128, 4, n).transpose(0, 1, 3, 2))
    if fmt == "e4m3":
        words = by_word.astype(ml_dtypes.float8_e4m3fn).view(np.uint8)
    else:
        c = by_word.astype(ml_dtypes.float4_e2m1fn).view(np.uint8) & 0xF
        words = (c[..., 0::2] | (c[..., 1::2] << 4)).reshape(k // 512, 128, 2 * n)
    return np.ascontiguousarray(words), np.ascontiguousarray(byte.astype(np.uint8).reshape(k // 512, 16, n))


def unpack_weight(words, scales, fmt):
    g, _, n = scales.shape
    words = np.ascontiguousarray(words).reshape(g, 128, n, -1)
    if fmt == "e4m3":
        vals = words.view(ml_dtypes.float8_e4m3fn).astype(np.float64)
    else:
        nib = np.empty((g, 128, n, 4), np.uint8)
        nib[..., 0::2] = words & 0xF
        nib[..., 1::2] = words >> 4
        vals = E2M1[nib]
    vals = vals * np.repeat(np.exp2(scales.astype(np.float64) - 127.0), 8, axis=1)[..., None]
    return vals.transpose(0, 1, 3, 2).reshape(g * 512, n)


def relu(v):
    return np.maximum(v, 0.0)


K, T, E, C, H, N = 512, 640, 5, 256, 512, 384


def by_expert(wq, xq):
    return np.concatenate([wq[e].T @ xq[:, e * C:(e + 1) * C] for e in range(E)], axis=1)


def setup_inputs():
    n = np.random.standard_normal
    s = mx_kscale(K)[:, None]
    u = mx_kscale(H)
    first = np.random.permutation(np.repeat(np.arange(E), T // E))
    second = (first + 1 + np.random.permutation(np.repeat(np.arange(E - 1), -(-T // (E - 1)))[:T])) % E
    while np.bincount(second, minlength=E).max() != T // E:
        load = np.bincount(second, minlength=E); hi, lo = int(load.argmax()), int(load.argmin())
        t = np.flatnonzero((second == hi) & (first != lo))[0]; second[t] = lo
    slot_token = np.empty(E * C, np.int64); pos = np.empty((2, T), np.int64); fill = np.zeros(E, np.int64)
    place = np.stack([np.random.permutation(C) for _ in range(E)])
    for r, deal in enumerate((first, second)):
        for t in np.random.permutation(T):
            e = deal[t]; j = e * C + place[e, fill[e]]; fill[e] += 1; slot_token[j] = t; pos[r, t] = j
    g = np.random.uniform(0.2, 0.8, T)
    x = pack_weight(n((K, T)) * s, "e4m3")
    return {
        "x_words": x[0],
        "x_scales": x[1],
        "w1": (n((E, K, H)) / np.sqrt(K) / s[None]).astype(np.float32),
        "w3": (n((E, K, H)) / np.sqrt(K) / s[None] * u[None, None, :]).astype(np.float32),
        "w2": (n((E, H, N)) / np.sqrt(H) / u[None, :, None]).astype(np.float32),
        "gate": np.stack([np.tile(g, (N, 1)), np.tile(1.0 - g, (N, 1))]).astype(np.float32),
        "offs": striped(slot_token),
        "pos1": striped(pos[0]),
        "pos2": striped(pos[1]),
    }


def reference(x_words, x_scales, w1, w3, w2, gate, offs, pos1, pos2):
    idx = unstriped(offs)
    xq = unpack_weight(x_words, x_scales, "e4m3")[:, idx]
    h = relu(by_expert(mxq(f64(w1), 1, "e4m3"), xq))
    h = h * by_expert(mxq(f64(w3), 1, "e4m3"), xq)
    y = by_expert(mxq(f64(w2), 1, "e4m3"), mxq(h, 0, "e4m3"))
    return f64(gate[0]) * y[:, unstriped(pos1)] + f64(gate[1]) * y[:, unstriped(pos2)]

@@ -1,0 +1,239 @@
+from contextlib import ExitStack
+
+import concourse.mybir as mybir
+
+K, T, E, C, H, N = 512, 640, 5, 256, 512, 384
+S = E * C
+FLOPS = 2 * S * (2 * K * H + H * N)
+BYTES = 4 * E * (2 * K * H + H * N) + K * T + (K // 32) * T + 4 * 2 * T + 2 * (S + 2 * T) + 4 * N * T
+
+F32 = mybir.dt.float32
+BF16 = mybir.dt.bfloat16
+I32 = mybir.dt.int32
+U32 = mybir.dt.uint32
+U16 = mybir.dt.uint16
+U8 = mybir.dt.uint8
+FP8X4 = mybir.dt.float8_e4m3fn_x4
+ALU = mybir.AluOpType
+
+P = 128
+PACK = 4
+LIST = 16
+HALF = C // 2
+BLOCKS = N // P
+EARLY = 3
+
+
+def tile_moe_pkd_glu_relu_kernel(
+    tc, x_words, x_scales, w1, w3, w2, gate, offs, pos1, pos2, out
+):
+    nc = tc.nc
+    with ExitStack() as ctx:
+        keep = ctx.enter_context(tc.tile_pool(name="keep", bufs=1))
+        ring = ctx.enter_context(tc.tile_pool(name="ring", bufs=4))
+        pair_ring = ctx.enter_context(tc.tile_pool(name="pair_ring", bufs=2))
+        psum_a = ctx.enter_context(tc.psum_pool(name="psum_a", bufs=3))
+        psum_b = ctx.enter_context(tc.psum_pool(name="psum_b", bufs=2))
+        psum_y = ctx.enter_context(tc.psum_pool(name="psum_y", bufs=3))
+
+        xw = keep.tile([P, T], I32, name="xw")
+        xs = keep.tile([P, T], U8, name="xs")
+        offs_t = keep.tile([P, S // LIST], U16, name="offs_t")
+        pos1_t = keep.tile([P, T // LIST], U16, name="pos1_t")
+        pos2_t = keep.tile([P, T // LIST], U16, name="pos2_t")
+        gate_t = keep.tile([P, 2, T], F32, name="gate_t")
+        nc.gpsimd.memset(xs[:].bitcast(I32), 0)
+        nc.sync.dma_start(out=xw[:], in_=x_words[0].rearrange("p t r -> p (t r)").bitcast(I32))
+        nc.sync.dma_start(out=offs_t[:], in_=offs)
+
+        raw13 = {}
+        for e in range(E):
+            for label, w in (("w3", w3), ("w1", w1)):
+                parts = 2 if (label, e) in (("w3", 0), ("w1", E - 1)) else 1
+                width = H // parts
+                raw13[label, e] = []
+                for q in range(parts):
+                    raw = keep.tile([P, PACK, width], F32, name=f"raw_{label}_{e}_{q}", tag=f"raw_{label}_{e}_{q}")
+                    nc.sync.dma_start(
+                        out=raw[:], in_=w[e, :, q * width : (q + 1) * width].rearrange("(p j) c -> p j c", j=PACK)
+                    )
+                    raw13[label, e].append(raw)
+                    if (label, e, q) == ("w3", 0, 0):
+                        for r in range(4):
+                            nc.sync.dma_start(out=xs[r:P:32, :].bitcast(I32), in_=x_scales[0, r:16:4, :].bitcast(I32))
+        raw2 = {}
+        for b in range(BLOCKS):
+            raw = keep.tile([P, E, PACK, P], F32, name=f"raw_w2_{b}")
+            for e in range(E):
+                nc.sync.dma_start(
+                    out=raw[:, e], in_=w2[e, :, b * P : (b + 1) * P].rearrange("(p j) n -> p j n", j=PACK)
+                )
+            raw2[b] = raw
+            if b == 0:
+                nc.sync.dma_start(out=pos1_t[:], in_=pos1)
+                nc.sync.dma_start(out=pos2_t[:], in_=pos2)
+                nc.sync.dma_start(out=gate_t[:], in_=gate[:, 0:P, :].rearrange("r p t -> p r t"))
+
+        xg_w, xg_s = {}, {}
+
+        def gather_tokens(e):
+            words = keep.tile([P, C], U32, name=f"xg_w{e}", tag=f"bf_w1_{e - EARLY}", align_bytes=64)
+            scales = keep.tile([P, C], U8, name=f"xg_s{e}", tag=f"bf_w3_{e - EARLY}", align_bytes=64)
+            lst = offs_t[:, e * C // LIST : (e + 1) * C // LIST]
+            nc.vector.tensor_copy(words[:], xw[:].bitcast(U32).indirect(lst))
+            nc.vector.tensor_copy(scales[:], xs[:].indirect(lst))
+            xg_w[e], xg_s[e] = words, scales
+
+        rounded, codes = {}, {}
+
+        def round13(label, e, u, on_vector):
+            if (label, e) not in rounded:
+                if e + EARLY < E:
+                    rounded[label, e] = keep.tile(
+                        [P, PACK, P, PACK], BF16, name=f"bf_{label}_{e}", tag=f"bf_{label}_{e}", align_bytes=64
+                    )
+                else:
+                    rounded[label, e] = pair_ring.tile([P, PACK, P, PACK], BF16, name="w13_bf", align_bytes=64)
+            parts = raw13[label, e]
+            width = P // len(parts)
+            for q, raw in enumerate(parts):
+                src = raw[:].rearrange("p j (m t) -> p m j t", t=PACK)[:, :, :, 2 * u : 2 * u + 2]
+                view = rounded[label, e][:, 2 * u : 2 * u + 2, q * width : (q + 1) * width, :].rearrange("p t m j -> p m j t")
+                if on_vector:
+                    nc.vector.tensor_copy(view, src)
+                else:
+                    nc.scalar.copy(view, src)
+
+        def quant13(label, e, calls):
+            words = ring.tile([P, H], U32, name="w13_words", align_bytes=64)
+            scales = ring.tile([P, H], U8, name="w13_scales", align_bytes=64)
+            flat = rounded[label, e][:].rearrange("p t m j -> p (t m j)")
+            width = H // calls
+            for q in reversed(range(calls)):
+                cols = slice(q * width, (q + 1) * width)
+                nc.vector.quantize_mx(
+                    out=words[:, cols].bitcast(FP8X4), scales=scales[:, cols],
+                    in_=flat[:, PACK * q * width : PACK * (q + 1) * width],
+                )
+            codes[label, e] = (words, scales)
+
+        banks = {}
+
+        def first_product(label, e):
+            pool = psum_a if label == "w1" else psum_b
+            words, scales = codes[label, e]
+            for s in range(2):
+                banks[label, e, s] = pool.tile([P, PACK, HALF], F32, name=f"bank_{label}")
+            for u in (1, 0):
+                for s in range(2):
+                    cols = slice(s * HALF, (s + 1) * HALF)
+                    for t in (2 * u, 2 * u + 1):
+                        m = slice(t * P, (t + 1) * P)
+                        nc.tensor.matmul_mx(
+                            out=banks[label, e, s][:, t, :], lhsT=words[:, m].bitcast(FP8X4), lhsT_scale=scales[:, m],
+                            rhs=xg_w[e][:, cols].bitcast(FP8X4), rhs_scale=xg_s[e][:, cols], start=True, stop=True,
+                        )
+
+        up = {}
+
+        def copy_up(e):
+            last = len(raw13["w1", e]) - 1
+            dst = keep.tile([P, 2, HALF, PACK], F32, name=f"up{e}", tag=f"raw_w1_{e}_{last}")
+            for s in range(2):
+                nc.scalar.copy(dst[:, s], banks["w3", e, s][:].rearrange("p t c -> p c t"))
+            up[e] = dst
+
+        h_bf, h_codes = {}, {}
+
+        def hidden(e):
+            dst = pair_ring.tile([P, 2, HALF, PACK], BF16, name="h_bf", align_bytes=64)
+            for s in range(2):
+                nc.vector.scalar_tensor_tensor(
+                    out=dst[:, s], in0=banks["w1", e, s][:].rearrange("p t c -> p c t"), scalar=0.0,
+                    in1=up[e][:, s], op0=ALU.max, op1=ALU.mult,
+                )
+            h_bf[e] = dst
+
+        def quant_h(e):
+            words = keep.tile([P, C], U32, name=f"h_words{e}", align_bytes=64)
+            scales = keep.tile([P, C], U8, name=f"h_scales{e}", align_bytes=64)
+            nc.vector.quantize_mx(
+                out=words[:].bitcast(FP8X4), scales=scales[:], in_=h_bf[e][:].rearrange("p s c t -> p (s c t)")
+            )
+            h_codes[e] = (words, scales)
+
+        gather_tokens(0)
+        gather_tokens(1)
+        gather_tokens(2)
+        for e in range(E):
+            round13("w3", e, 0, False)
+            round13("w3", e, 1, e not in (1, 2))
+            if e >= 1:
+                hidden(e - 1)
+            quant13("w3", e, 2)
+            if e >= 1:
+                quant_h(e - 1)
+            first_product("w3", e)
+            round13("w1", e, 0, False)
+            round13("w1", e, 1, True)
+            copy_up(e)
+            quant13("w1", e, 2)
+            first_product("w1", e)
+            if e + 3 < E:
+                gather_tokens(e + 3)
+        hidden(E - 1)
+        quant_h(E - 1)
+
+        w2_codes = {}
+
+        def prepare_w2(b):
+            words = keep.tile([P, E * P], U32, name=f"w2_words{b}", align_bytes=64)
+            scales = keep.tile([P, E * P], U8, name=f"w2_scales{b}", align_bytes=64)
+            for e0, e1 in ((0, 2), (2, 4), (4, 5)):
+                dst = keep.tile([P, e1 - e0, P, PACK], BF16, name=f"w2_bf{b}_{e0}", tag=f"shared{b}_{e0}", align_bytes=64)
+                nc.scalar.copy(
+                    dst[:].rearrange("p e (c i) j -> p e c j i", i=4),
+                    raw2[b][:, e0:e1].rearrange("p e j (c i) -> p e c j i", i=4),
+                )
+                cols = slice(e0 * P, e1 * P)
+                nc.vector.quantize_mx(
+                    out=words[:, cols].bitcast(FP8X4), scales=scales[:, cols],
+                    in_=dst[:].rearrange("p e n j -> p (e n j)"),
+                )
+            w2_codes[b] = (words, scales)
+
+        def second_product(b):
+            y = keep.tile([P, S], F32, name=f"y{b}")
+            for e0 in range(0, E, 2):
+                pair = list(range(e0, min(e0 + 2, E)))
+                bank = psum_y.tile([P, 2 * C], F32, name="bank_y")
+                for e in pair:
+                    words, scales = w2_codes[b]
+                    m = slice(e * P, (e + 1) * P)
+                    nc.tensor.matmul_mx(
+                        out=bank[:, (e - e0) * C : (e - e0 + 1) * C], lhsT=words[:, m].bitcast(FP8X4), lhsT_scale=scales[:, m],
+                        rhs=h_codes[e][0][:].bitcast(FP8X4), rhs_scale=h_codes[e][1][:], start=True, stop=True,
+                    )
+                width = len(pair) * C
+                nc.scalar.copy(y[:, e0 * C : e0 * C + width], bank[:, 0:width])
+            return y
+
+        def combine(b, y, pieces):
+            width = T // pieces
+            for q in range(pieces):
+                tok = slice(q * width, (q + 1) * width)
+                lst = slice(q * width // LIST, (q + 1) * width // LIST)
+                first = pair_ring.tile([P, width], F32, name="first")
+                second = keep.tile([P, width], F32, name=f"second{b}_{q}", tag=f"shared{b + 1 + q}_0", align_bytes=64)
+                total = keep.tile([P, width], F32, name=f"total{b}_{q}", tag=f"shared{b + 1 + q}_2", align_bytes=64)
+                nc.vector.tensor_tensor(first[:], y[:].indirect(pos1_t[:, lst]), gate_t[:, 0, tok], ALU.mult)
+                nc.vector.tensor_tensor(second[:], y[:].indirect(pos2_t[:, lst]), gate_t[:, 1, tok], ALU.mult)
+                nc.vector.tensor_tensor(total[:], first[:], second[:], ALU.add)
+                nc.sync.dma_start(out=out[b * P : (b + 1) * P, tok], in_=total[:])
+
+        prepare_w2(0)
+        for b in range(BLOCKS):
+            y = second_product(b)
+            if b + 1 < BLOCKS:
+                prepare_w2(b + 1)
+            combine(b, y, 2 if b == BLOCKS - 1 else 1)

@@ -22,6 +22,9 @@ LIST = 16
 HALF = C // 2
 BLOCKS = N // P
 EARLY = 3
+GROUPS = ((0, 2), (2, 4), (4, 5))
+WHOLE = 0
+LAST_PIECES = (320,320,)
 
 
 def tile_moe_pkd_glu_relu_kernel(
@@ -30,18 +33,20 @@ def tile_moe_pkd_glu_relu_kernel(
     nc = tc.nc
     with ExitStack() as ctx:
         keep = ctx.enter_context(tc.tile_pool(name="keep", bufs=1))
-        ring = ctx.enter_context(tc.tile_pool(name="ring", bufs=4))
-        pair_ring = ctx.enter_context(tc.tile_pool(name="pair_ring", bufs=2))
-        psum_a = ctx.enter_context(tc.psum_pool(name="psum_a", bufs=3))
-        psum_b = ctx.enter_context(tc.psum_pool(name="psum_b", bufs=2))
-        psum_y = ctx.enter_context(tc.psum_pool(name="psum_y", bufs=3))
+        ring = ctx.enter_context(tc.tile_pool(name="ring", bufs=2))
+        low_ring = ctx.enter_context(tc.tile_pool(name="low_ring", bufs=1))
+        psum = ctx.enter_context(tc.psum_pool(name="psum", bufs=1))
+        psum_y = ctx.enter_context(tc.psum_pool(name="psum_y", bufs=2))
 
-        xw = keep.tile([P, T], I32, name="xw")
-        xs = keep.tile([P, T], U8, name="xs")
+        def held(shape, dtype, name, tag=None):
+            return keep.tile(shape, dtype, name=name, tag=tag or name, align_bytes=64)
+
+        xw = held([P, T], I32, "xw")
+        xs = held([P, T], U8, "xs")
         offs_t = keep.tile([P, S // LIST], U16, name="offs_t")
         pos1_t = keep.tile([P, T // LIST], U16, name="pos1_t")
         pos2_t = keep.tile([P, T // LIST], U16, name="pos2_t")
-        gate_t = keep.tile([P, 2, T], F32, name="gate_t")
+        gates = [held([P, T], F32, f"gate{r}") for r in range(2)]
         nc.gpsimd.memset(xs[:].bitcast(I32), 0)
         nc.sync.dma_start(out=xw[:], in_=x_words[0].rearrange("p t r -> p (t r)").bitcast(I32))
         nc.sync.dma_start(out=offs_t[:], in_=offs)
@@ -49,152 +54,175 @@ def tile_moe_pkd_glu_relu_kernel(
         raw13 = {}
         for e in range(E):
             for label, w in (("w3", w3), ("w1", w1)):
-                parts = 2 if (label, e) in (("w3", 0), ("w1", E - 1)) else 1
+                parts = 2 if (label, e) in (("w3", 0), ) else 1
                 width = H // parts
                 raw13[label, e] = []
                 for q in range(parts):
-                    raw = keep.tile([P, PACK, width], F32, name=f"raw_{label}_{e}_{q}", tag=f"raw_{label}_{e}_{q}")
+                    raw = held([P, PACK, width], F32, f"raw_{label}_{e}_{q}")
                     nc.sync.dma_start(
                         out=raw[:], in_=w[e, :, q * width : (q + 1) * width].rearrange("(p j) c -> p j c", j=PACK)
                     )
                     raw13[label, e].append(raw)
+                    if (label, e, q) == None:
+                        nc.sync.dma_start(out=pos1_t[:], in_=pos1)
+                        nc.sync.dma_start(out=gates[0][:], in_=gate[0, 0:P, :])
+                    if (label, e, q) == None:
+                        nc.sync.dma_start(out=pos2_t[:], in_=pos2)
+                        nc.sync.dma_start(out=gates[1][:], in_=gate[1, 0:P, :])
                     if (label, e, q) == ("w3", 0, 0):
                         for r in range(4):
                             nc.sync.dma_start(out=xs[r:P:32, :].bitcast(I32), in_=x_scales[0, r:16:4, :].bitcast(I32))
         raw2 = {}
         for b in range(BLOCKS):
-            raw = keep.tile([P, E, PACK, P], F32, name=f"raw_w2_{b}")
-            for e in range(E):
-                nc.sync.dma_start(
-                    out=raw[:, e], in_=w2[e, :, b * P : (b + 1) * P].rearrange("(p j) n -> p j n", j=PACK)
-                )
-            raw2[b] = raw
-            if b == 0:
+            for e0, e1 in GROUPS:
+                if e1 <= WHOLE:
+                    if b == 0:
+                        raw = held([P, e1 - e0, PACK, N], F32, f"raw_w2_{e0}")
+                        for e in range(e0, e1):
+                            nc.sync.dma_start(out=raw[:, e - e0], in_=w2[e].rearrange("(p j) n -> p j n", j=PACK))
+                        for c in range(BLOCKS):
+                            raw2[c, e0] = raw[:, :, :, c * P : (c + 1) * P]
+                    continue
+                raw = held([P, e1 - e0, PACK, P], F32, f"raw_w2_{b}_{e0}")
+                for e in range(e0, e1):
+                    nc.sync.dma_start(
+                        out=raw[:, e - e0], in_=w2[e, :, b * P : (b + 1) * P].rearrange("(p j) n -> p j n", j=PACK)
+                    )
+                raw2[b, e0] = raw[:]
+            if b == 0 and None is None:
                 nc.sync.dma_start(out=pos1_t[:], in_=pos1)
+                nc.sync.dma_start(out=gates[0][:], in_=gate[0, 0:P, :])
+            if b == 0 and None is None:
                 nc.sync.dma_start(out=pos2_t[:], in_=pos2)
-                nc.sync.dma_start(out=gate_t[:], in_=gate[:, 0:P, :].rearrange("r p t -> p r t"))
+                nc.sync.dma_start(out=gates[1][:], in_=gate[1, 0:P, :])
 
         xg_w, xg_s = {}, {}
 
-        def gather_tokens(e):
-            words = keep.tile([P, C], U32, name=f"xg_w{e}", tag=f"bf_w1_{e - EARLY}", align_bytes=64)
-            scales = keep.tile([P, C], U8, name=f"xg_s{e}", tag=f"bf_w3_{e - EARLY}", align_bytes=64)
-            lst = offs_t[:, e * C // LIST : (e + 1) * C // LIST]
-            nc.vector.tensor_copy(words[:], xw[:].bitcast(U32).indirect(lst))
-            nc.vector.tensor_copy(scales[:], xs[:].indirect(lst))
-            xg_w[e], xg_s[e] = words, scales
+        def gather_words(e, tag=None):
+            xg_w[e] = held([P, C], U32, f"xg_w{e}", tag)
+            nc.vector.tensor_copy(xg_w[e][:], xw[:].bitcast(U32).indirect(offs_t[:, e * C // LIST : (e + 1) * C // LIST]))
+
+        def gather_scales(e, tag=None):
+            xg_s[e] = held([P, C], U8, f"xg_s{e}", tag)
+            nc.vector.tensor_copy(xg_s[e][:], xs[:].indirect(offs_t[:, e * C // LIST : (e + 1) * C // LIST]))
 
         rounded, codes = {}, {}
 
-        def round13(label, e, u, on_vector):
-            if (label, e) not in rounded:
-                if e + EARLY < E:
-                    rounded[label, e] = keep.tile(
-                        [P, PACK, P, PACK], BF16, name=f"bf_{label}_{e}", tag=f"bf_{label}_{e}", align_bytes=64
-                    )
-                else:
-                    rounded[label, e] = pair_ring.tile([P, PACK, P, PACK], BF16, name="w13_bf", align_bytes=64)
+        def round13(label, e, q, on_vector):
             parts = raw13[label, e]
-            width = P // len(parts)
-            for q, raw in enumerate(parts):
-                src = raw[:].rearrange("p j (m t) -> p m j t", t=PACK)[:, :, :, 2 * u : 2 * u + 2]
-                view = rounded[label, e][:, 2 * u : 2 * u + 2, q * width : (q + 1) * width, :].rearrange("p t m j -> p m j t")
+            cut = P // 2 if len(parts) == 2 else (80 if e == E - 1 else 80)
+            m = slice(0, cut) if q == 0 else slice(cut, P)
+            raw = parts[q][:] if len(parts) == 2 else parts[0][:, :, PACK * m.start : PACK * m.stop]
+            for u in (1, 0):
+                if (label, e, u) not in rounded:
+                    rounded[label, e, u] = low_ring.tile([P, 2, P, PACK], BF16, name=f"bf_{label}_{u}", align_bytes=64)
+                src = raw.rearrange("p j (m t) -> p m j t", t=PACK)[:, :, :, 2 * u : 2 * u + 2]
+                view = rounded[label, e, u][:, :, m, :].rearrange("p t m j -> p m j t")
                 if on_vector:
                     nc.vector.tensor_copy(view, src)
                 else:
                     nc.scalar.copy(view, src)
 
-        def quant13(label, e, calls):
-            words = ring.tile([P, H], U32, name="w13_words", align_bytes=64)
-            scales = ring.tile([P, H], U8, name="w13_scales", align_bytes=64)
-            flat = rounded[label, e][:].rearrange("p t m j -> p (t m j)")
-            width = H // calls
-            for q in reversed(range(calls)):
-                cols = slice(q * width, (q + 1) * width)
-                nc.vector.quantize_mx(
-                    out=words[:, cols].bitcast(FP8X4), scales=scales[:, cols],
-                    in_=flat[:, PACK * q * width : PACK * (q + 1) * width],
-                )
-            codes[label, e] = (words, scales)
+        def quant13(label, e, u):
+            words = ring.tile([P, 2 * P], U32, name=f"words_{label}_{u}", align_bytes=64)
+            scales = ring.tile([P, 2 * P], U8, name=f"scales_{label}_{u}", align_bytes=64)
+            nc.vector.quantize_mx(
+                out=words[:].bitcast(FP8X4), scales=scales[:],
+                in_=rounded[label, e, u][:].rearrange("p t m j -> p (t m j)"),
+            )
+            codes[label, e, u] = (words, scales)
 
         banks = {}
 
         def first_product(label, e):
-            pool = psum_a if label == "w1" else psum_b
-            words, scales = codes[label, e]
             for s in range(2):
-                banks[label, e, s] = pool.tile([P, PACK, HALF], F32, name=f"bank_{label}")
+                turn = (e + (label == "w1")) % 2
+                banks[label, e, s] = psum.tile([P, PACK, HALF], F32, name=f"bank_{label}", tag=f"bank{turn}_{s}")
             for u in (1, 0):
+                words, scales = codes[label, e, u]
                 for s in range(2):
                     cols = slice(s * HALF, (s + 1) * HALF)
-                    for t in (2 * u, 2 * u + 1):
+                    for t in range(2):
                         m = slice(t * P, (t + 1) * P)
                         nc.tensor.matmul_mx(
-                            out=banks[label, e, s][:, t, :], lhsT=words[:, m].bitcast(FP8X4), lhsT_scale=scales[:, m],
+                            out=banks[label, e, s][:, 2 * u + t, :],
+                            lhsT=words[:, m].bitcast(FP8X4), lhsT_scale=scales[:, m],
                             rhs=xg_w[e][:, cols].bitcast(FP8X4), rhs_scale=xg_s[e][:, cols], start=True, stop=True,
                         )
 
         up = {}
 
         def copy_up(e):
-            last = len(raw13["w1", e]) - 1
-            dst = keep.tile([P, 2, HALF, PACK], F32, name=f"up{e}", tag=f"raw_w1_{e}_{last}")
             for s in range(2):
-                nc.scalar.copy(dst[:, s], banks["w3", e, s][:].rearrange("p t c -> p c t"))
-            up[e] = dst
+                up[e, s] = raw13["w1", e][0][:, 2 * s : 2 * s + 2, 0 : H // 2].rearrange("p r (c t) -> p r c t", t=PACK)
+                nc.scalar.copy(up[e, s], banks["w3", e, s][:].rearrange("p t (r c) -> p r c t", r=2))
 
         h_bf, h_codes = {}, {}
 
-        def hidden(e):
-            dst = pair_ring.tile([P, 2, HALF, PACK], BF16, name="h_bf", align_bytes=64)
-            for s in range(2):
-                nc.vector.scalar_tensor_tensor(
-                    out=dst[:, s], in0=banks["w1", e, s][:].rearrange("p t c -> p c t"), scalar=0.0,
-                    in1=up[e][:, s], op0=ALU.max, op1=ALU.mult,
-                )
-            h_bf[e] = dst
+        def hidden(e, s):
+            if s == 0:
+                tag = f"raw_w3_{e + 1}_0" if e + 1 < E and e + 1 + EARLY >= E and False else None
+                h_bf[e] = held([P, 2, HALF, PACK], BF16, f"h_bf{e}", tag)
+            nc.vector.scalar_tensor_tensor(
+                out=h_bf[e][:, s].rearrange("p (r c) t -> p r c t", r=2),
+                in0=banks["w1", e, s][:].rearrange("p t (r c) -> p r c t", r=2), scalar=0.0,
+                in1=up[e, s], op0=ALU.max, op1=ALU.mult,
+            )
 
         def quant_h(e):
-            words = keep.tile([P, C], U32, name=f"h_words{e}", align_bytes=64)
-            scales = keep.tile([P, C], U8, name=f"h_scales{e}", align_bytes=64)
+            words = held([P, C], U32, f"h_words{e}")
+            scales = held([P, C], U8, f"h_scales{e}")
             nc.vector.quantize_mx(
                 out=words[:].bitcast(FP8X4), scales=scales[:], in_=h_bf[e][:].rearrange("p s c t -> p (s c t)")
             )
             h_codes[e] = (words, scales)
 
-        gather_tokens(0)
-        gather_tokens(1)
-        gather_tokens(2)
+        for e in range(EARLY):
+            gather_words(e)
+        for e in range(EARLY):
+            gather_scales(e)
         for e in range(E):
             round13("w3", e, 0, False)
-            round13("w3", e, 1, e not in (1, 2))
+            round13("w3", e, 1, e not in (0,))
+            quant13("w3", e, 1)
+            quant13("w3", e, 0)
             if e >= 1:
-                hidden(e - 1)
-            quant13("w3", e, 2)
-            if e >= 1:
-                quant_h(e - 1)
+                hidden(e - 1, 0)
             first_product("w3", e)
             round13("w1", e, 0, False)
             round13("w1", e, 1, True)
+            if e >= 1:
+                hidden(e - 1, 1)
             copy_up(e)
-            quant13("w1", e, 2)
+            quant13("w1", e, 1)
+            quant13("w1", e, 0)
+            if e >= 1:
+                quant_h(e - 1)
             first_product("w1", e)
-            if e + 3 < E:
-                gather_tokens(e + 3)
-        hidden(E - 1)
+            if e + EARLY < E:
+                gather_words(e + EARLY, f"raw_w1_{e}_0")
+                gather_scales(e + EARLY, f"raw_w3_{e}_1" if e == 0 else f"raw_w3_{e}_0")
+        hidden(E - 1, 0)
+        hidden(E - 1, 1)
         quant_h(E - 1)
 
-        w2_codes = {}
+        w2_codes, w2_tag = {}, {}
 
         def prepare_w2(b):
-            words = keep.tile([P, E * P], U32, name=f"w2_words{b}", align_bytes=64)
-            scales = keep.tile([P, E * P], U8, name=f"w2_scales{b}", align_bytes=64)
-            for e0, e1 in ((0, 2), (2, 4), (4, 5)):
-                dst = keep.tile([P, e1 - e0, P, PACK], BF16, name=f"w2_bf{b}_{e0}", tag=f"shared{b}_{e0}", align_bytes=64)
-                nc.scalar.copy(
-                    dst[:].rearrange("p e (c i) j -> p e c j i", i=4),
-                    raw2[b][:, e0:e1].rearrange("p e j (c i) -> p e c j i", i=4),
-                )
+            words = held([P, E * P], U32, f"w2_words{b}")
+            scales = held([P, E * P], U8, f"w2_scales{b}")
+            for g, (e0, e1) in enumerate(GROUPS):
+                tag = f"w2_words{b - 1}" if (b, g) in ((1, 0), ) else f"shared{b}_{g}"
+                if (b, g) == (0, 0) and None:
+                    tag = None
+                w2_tag[b, g] = tag
+                dst = held([P, e1 - e0, P, PACK], BF16, f"w2_bf{b}_{g}", tag)
+                view = dst[:].rearrange("p e (c i) j -> p e c j i", i=4)
+                src = raw2[b, e0].rearrange("p e j (c i) -> p e c j i", i=4)
+                if b == 0 and g in (1,):
+                    nc.vector.tensor_copy(view, src)
+                else:
+                    nc.scalar.copy(view, src)
                 cols = slice(e0 * P, e1 * P)
                 nc.vector.quantize_mx(
                     out=words[:, cols].bitcast(FP8X4), scales=scales[:, cols],
@@ -203,31 +231,34 @@ def tile_moe_pkd_glu_relu_kernel(
             w2_codes[b] = (words, scales)
 
         def second_product(b):
-            y = keep.tile([P, S], F32, name=f"y{b}")
-            for e0 in range(0, E, 2):
-                pair = list(range(e0, min(e0 + 2, E)))
+            y = held([P, S], F32, f"y{b}")
+            words, scales = w2_codes[b]
+            for g, (e0, e1) in enumerate(GROUPS):
                 bank = psum_y.tile([P, 2 * C], F32, name="bank_y")
-                for e in pair:
-                    words, scales = w2_codes[b]
+                for e in range(e0, e1):
                     m = slice(e * P, (e + 1) * P)
                     nc.tensor.matmul_mx(
                         out=bank[:, (e - e0) * C : (e - e0 + 1) * C], lhsT=words[:, m].bitcast(FP8X4), lhsT_scale=scales[:, m],
                         rhs=h_codes[e][0][:].bitcast(FP8X4), rhs_scale=h_codes[e][1][:], start=True, stop=True,
                     )
-                width = len(pair) * C
-                nc.scalar.copy(y[:, e0 * C : e0 * C + width], bank[:, 0:width])
+                if b == 0 and g in ():
+                    nc.vector.tensor_copy(y[:, e0 * C : e1 * C], bank[:, 0 : (e1 - e0) * C])
+                else:
+                    nc.scalar.copy(y[:, e0 * C : e1 * C], bank[:, 0 : (e1 - e0) * C])
             return y
 
-        def combine(b, y, pieces):
-            width = T // pieces
-            for q in range(pieces):
-                tok = slice(q * width, (q + 1) * width)
-                lst = slice(q * width // LIST, (q + 1) * width // LIST)
-                first = pair_ring.tile([P, width], F32, name="first")
-                second = keep.tile([P, width], F32, name=f"second{b}_{q}", tag=f"shared{b + 1 + q}_0", align_bytes=64)
-                total = keep.tile([P, width], F32, name=f"total{b}_{q}", tag=f"shared{b + 1 + q}_2", align_bytes=64)
-                nc.vector.tensor_tensor(first[:], y[:].indirect(pos1_t[:, lst]), gate_t[:, 0, tok], ALU.mult)
-                nc.vector.tensor_tensor(second[:], y[:].indirect(pos2_t[:, lst]), gate_t[:, 1, tok], ALU.mult)
+        def combine(b, y, widths):
+            t0 = 0
+            for q, width in enumerate(widths):
+                tok = slice(t0, t0 + width)
+                lst = slice(t0 // LIST, (t0 + width) // LIST)
+                t0 = t0 + width
+                behind = b + 1 < BLOCKS
+                first = held([P, width], F32, f"first{b}_{q}", f"first{q}")
+                second = held([P, width], F32, f"second{b}_{q}", w2_tag[b + 1, 1] if behind else None)
+                total = held([P, width], F32, f"total{b}_{q}", f"shared{b + 1}_2" if behind else None)
+                nc.vector.tensor_tensor(first[:], y[:].indirect(pos1_t[:, lst]), gates[0][:, tok], ALU.mult)
+                nc.vector.tensor_tensor(second[:], y[:].indirect(pos2_t[:, lst]), gates[1][:, tok], ALU.mult)
                 nc.vector.tensor_tensor(total[:], first[:], second[:], ALU.add)
                 nc.sync.dma_start(out=out[b * P : (b + 1) * P, tok], in_=total[:])
 
@@ -236,4 +267,4 @@ def tile_moe_pkd_glu_relu_kernel(
             y = second_product(b)
             if b + 1 < BLOCKS:
                 prepare_w2(b + 1)
-            combine(b, y, 2 if b == BLOCKS - 1 else 1)
+            combine(b, y, LAST_PIECES if b == BLOCKS - 1 else (T,))

@@ -1,6 +1,7 @@
 from contextlib import ExitStack
 
 import concourse.mybir as mybir
+from concourse.masks import make_identity
 
 K, T, E, C, H, N = 512, 640, 5, 256, 512, 384
 S = E * C
@@ -24,7 +25,7 @@ BLOCKS = N // P
 EARLY = 3
 GROUPS = ((0, 2), (2, 4), (4, 5))
 WHOLE = 0
-LAST_PIECES = (320,320,)
+LAST_PIECES = (448,192,)
 
 
 def tile_moe_pkd_glu_relu_kernel(
@@ -34,9 +35,9 @@ def tile_moe_pkd_glu_relu_kernel(
     with ExitStack() as ctx:
         keep = ctx.enter_context(tc.tile_pool(name="keep", bufs=1))
         ring = ctx.enter_context(tc.tile_pool(name="ring", bufs=2))
-        low_ring = ctx.enter_context(tc.tile_pool(name="low_ring", bufs=1))
+        low_ring = ctx.enter_context(tc.tile_pool(name="low_ring", bufs=2))
         psum = ctx.enter_context(tc.psum_pool(name="psum", bufs=1))
-        psum_y = ctx.enter_context(tc.psum_pool(name="psum_y", bufs=2))
+        psum_y = ctx.enter_context(tc.psum_pool(name="psum_y", bufs=4))
 
         def held(shape, dtype, name, tag=None):
             return keep.tile(shape, dtype, name=name, tag=tag or name, align_bytes=64)
@@ -51,6 +52,8 @@ def tile_moe_pkd_glu_relu_kernel(
         nc.sync.dma_start(out=xw[:], in_=x_words[0].rearrange("p t r -> p (t r)").bitcast(I32))
         nc.sync.dma_start(out=offs_t[:], in_=offs)
 
+        ident = held([P, P], F32, "ident")
+        make_identity(nc, ident[:])
         raw13 = {}
         for e in range(E):
             for label, w in (("w3", w3), ("w1", w1)):
@@ -113,24 +116,29 @@ def tile_moe_pkd_glu_relu_kernel(
             cut = P // 2 if len(parts) == 2 else (80 if e == E - 1 else 80)
             m = slice(0, cut) if q == 0 else slice(cut, P)
             raw = parts[q][:] if len(parts) == 2 else parts[0][:, :, PACK * m.start : PACK * m.stop]
-            for u in (1, 0):
-                if (label, e, u) not in rounded:
-                    rounded[label, e, u] = low_ring.tile([P, 2, P, PACK], BF16, name=f"bf_{label}_{u}", align_bytes=64)
-                src = raw.rearrange("p j (m t) -> p m j t", t=PACK)[:, :, :, 2 * u : 2 * u + 2]
-                view = rounded[label, e, u][:, :, m, :].rearrange("p t m j -> p m j t")
+            if (label, e) not in rounded:
+                rounded[label, e] = low_ring.tile([P, PACK, P, PACK], BF16, name=f"bf_{label}", align_bytes=64)
+            for ts in quarters(label, e):
+                src = raw.rearrange("p j (m t) -> p m j t", t=PACK)[:, :, :, ts]
+                view = rounded[label, e][:, ts, m, :].rearrange("p t m j -> p m j t")
                 if on_vector:
                     nc.vector.tensor_copy(view, src)
                 else:
                     nc.scalar.copy(view, src)
 
-        def quant13(label, e, u):
-            words = ring.tile([P, 2 * P], U32, name=f"words_{label}_{u}", align_bytes=64)
-            scales = ring.tile([P, 2 * P], U8, name=f"scales_{label}_{u}", align_bytes=64)
-            nc.vector.quantize_mx(
-                out=words[:].bitcast(FP8X4), scales=scales[:],
-                in_=rounded[label, e, u][:].rearrange("p t m j -> p (t m j)"),
-            )
-            codes[label, e, u] = (words, scales)
+        def quarters(label, e):
+            return (slice(2, 4), slice(0, 2)) if (label, e) in tuple((a, b) for a in ("w1", "w3") for b in range(E)) else (slice(0, 4),)
+
+        def quant13(label, e):
+            words = ring.tile([P, H], U32, name=f"words_{label}", align_bytes=64)
+            scales = ring.tile([P, H], U8, name=f"scales_{label}", align_bytes=64)
+            for ts in quarters(label, e):
+                cols = slice(ts.start * P, ts.stop * P)
+                nc.vector.quantize_mx(
+                    out=words[:, cols].bitcast(FP8X4), scales=scales[:, cols],
+                    in_=rounded[label, e][:, ts].rearrange("p t m j -> p (t m j)"),
+                )
+            codes[label, e] = (words, scales)
 
         banks = {}
 
@@ -138,14 +146,14 @@ def tile_moe_pkd_glu_relu_kernel(
             for s in range(2):
                 turn = (e + (label == "w1")) % 2
                 banks[label, e, s] = psum.tile([P, PACK, HALF], F32, name=f"bank_{label}", tag=f"bank{turn}_{s}")
-            for u in (1, 0):
-                words, scales = codes[label, e, u]
+            words, scales = codes[label, e]
+            for ts in quarters(label, e):
                 for s in range(2):
                     cols = slice(s * HALF, (s + 1) * HALF)
-                    for t in range(2):
+                    for t in range(ts.start, ts.stop):
                         m = slice(t * P, (t + 1) * P)
                         nc.tensor.matmul_mx(
-                            out=banks[label, e, s][:, 2 * u + t, :],
+                            out=banks[label, e, s][:, t, :],
                             lhsT=words[:, m].bitcast(FP8X4), lhsT_scale=scales[:, m],
                             rhs=xg_w[e][:, cols].bitcast(FP8X4), rhs_scale=xg_s[e][:, cols], start=True, stop=True,
                         )
@@ -184,8 +192,7 @@ def tile_moe_pkd_glu_relu_kernel(
         for e in range(E):
             round13("w3", e, 0, False)
             round13("w3", e, 1, e not in (0,))
-            quant13("w3", e, 1)
-            quant13("w3", e, 0)
+            quant13("w3", e)
             if e >= 1:
                 hidden(e - 1, 0)
             first_product("w3", e)
@@ -194,8 +201,7 @@ def tile_moe_pkd_glu_relu_kernel(
             if e >= 1:
                 hidden(e - 1, 1)
             copy_up(e)
-            quant13("w1", e, 1)
-            quant13("w1", e, 0)
+            quant13("w1", e)
             if e >= 1:
                 quant_h(e - 1)
             first_product("w1", e)
@@ -211,15 +217,19 @@ def tile_moe_pkd_glu_relu_kernel(
         def prepare_w2(b):
             words = held([P, E * P], U32, f"w2_words{b}")
             scales = held([P, E * P], U8, f"w2_scales{b}")
-            for g, (e0, e1) in enumerate(GROUPS):
+            for g in ((0,1,2) if b == 0 else (0, 1, 2)):
+                e0, e1 = GROUPS[g]
                 tag = f"w2_words{b - 1}" if (b, g) in ((1, 0), ) else f"shared{b}_{g}"
                 if (b, g) == (0, 0) and None:
                     tag = None
                 w2_tag[b, g] = tag
-                dst = held([P, e1 - e0, P, PACK], BF16, f"w2_bf{b}_{g}", tag)
+                if (b, g) in ():
+                    dst = low_ring.tile([P, e1 - e0, P, PACK], BF16, name=f"w2_bf{b}_{g}", tag="bf_w1", align_bytes=64)
+                else:
+                    dst = held([P, e1 - e0, P, PACK], BF16, f"w2_bf{b}_{g}", tag)
                 view = dst[:].rearrange("p e (c i) j -> p e c j i", i=4)
                 src = raw2[b, e0].rearrange("p e j (c i) -> p e c j i", i=4)
-                if b == 0 and g in (1,):
+                if (b == 0 and g in (1,)) or (b, g) in ():
                     nc.vector.tensor_copy(view, src)
                 else:
                     nc.scalar.copy(view, src)
@@ -233,7 +243,8 @@ def tile_moe_pkd_glu_relu_kernel(
         def second_product(b):
             y = held([P, S], F32, f"y{b}")
             words, scales = w2_codes[b]
-            for g, (e0, e1) in enumerate(GROUPS):
+            for g in ((0,1,2) if b == 0 else (0, 1, 2)):
+                e0, e1 = GROUPS[g]
                 bank = psum_y.tile([P, 2 * C], F32, name="bank_y")
                 for e in range(e0, e1):
                     m = slice(e * P, (e + 1) * P)
@@ -241,11 +252,28 @@ def tile_moe_pkd_glu_relu_kernel(
                         out=bank[:, (e - e0) * C : (e - e0 + 1) * C], lhsT=words[:, m].bitcast(FP8X4), lhsT_scale=scales[:, m],
                         rhs=h_codes[e][0][:].bitcast(FP8X4), rhs_scale=h_codes[e][1][:], start=True, stop=True,
                     )
-                if b == 0 and g in ():
+                if g in (() if b == 0 else ()):
                     nc.vector.tensor_copy(y[:, e0 * C : e1 * C], bank[:, 0 : (e1 - e0) * C])
                 else:
                     nc.scalar.copy(y[:, e0 * C : e1 * C], bank[:, 0 : (e1 - e0) * C])
             return y
+
+        def add_by_transposes(total, first, second):
+            turned = held([P, T], F32, "turned")
+            for c0, c1 in ((0, 3), (3, 5)):
+                bank = psum.tile([P, c1 - c0, P], F32, name="bank_turn", tag=f"bank0_{c0 // 3}")
+                for c in range(c0, c1):
+                    for k, src in enumerate((first, second)):
+                        nc.tensor.matmul(
+                            bank[:, c - c0, :], src[:, c * P : (c + 1) * P], ident[:],
+                            is_transpose=True, start=k == 0, stop=k == 1,
+                        )
+                nc.scalar.copy(turned[:, c0 * P : c1 * P], bank[:].rearrange("p c n -> p (c n)"))
+            for c0, c1 in ((0, 3), (3, 5)):
+                bank = psum.tile([P, c1 - c0, P], F32, name="bank_back", tag=f"bank1_{c0 // 3}")
+                for c in range(c0, c1):
+                    nc.tensor.transpose(bank[:, c - c0, :], turned[:, c * P : (c + 1) * P], ident[:])
+                nc.scalar.copy(total[:, c0 * P : c1 * P], bank[:].rearrange("p c n -> p (c n)"))
 
         def combine(b, y, widths):
             t0 = 0
@@ -254,13 +282,17 @@ def tile_moe_pkd_glu_relu_kernel(
                 lst = slice(t0 // LIST, (t0 + width) // LIST)
                 t0 = t0 + width
                 behind = b + 1 < BLOCKS
-                first = held([P, width], F32, f"first{b}_{q}", f"first{q}")
-                second = held([P, width], F32, f"second{b}_{q}", w2_tag[b + 1, 1] if behind else None)
-                total = held([P, width], F32, f"total{b}_{q}", f"shared{b + 1}_2" if behind else None)
+                first = held([P, width], F32, f"first{b}_{q}")
+                second = held([P, width], F32, f"second{b}_{q}", w2_tag.get((b + 1, (1,2)[b])) if behind else None)
+                total = held([P, width], F32, f"total{b}_{q}", w2_tag.get((b + 1, (2,9)[b])) if behind else None)
                 nc.vector.tensor_tensor(first[:], y[:].indirect(pos1_t[:, lst]), gates[0][:, tok], ALU.mult)
                 nc.vector.tensor_tensor(second[:], y[:].indirect(pos2_t[:, lst]), gates[1][:, tok], ALU.mult)
-                nc.vector.tensor_tensor(total[:], first[:], second[:], ALU.add)
-                nc.sync.dma_start(out=out[b * P : (b + 1) * P, tok], in_=total[:])
+                if b == 1 and True:
+                    add_by_transposes(total, first, second)
+                else:
+                    nc.vector.tensor_tensor(total[:], first[:], second[:], ALU.add)
+                queue = nc.scalar if b == 1 and True else nc.sync
+                queue.dma_start(out=out[b * P : (b + 1) * P, tok], in_=total[:])
 
         prepare_w2(0)
         for b in range(BLOCKS):

@@ -113,7 +113,7 @@ def tile_moe_pkd_glu_relu_kernel(
 
         def round13(label, e, q, on_vector):
             parts = raw13[label, e]
-            cut = P // 2 if len(parts) == 2 else (80 if e == E - 1 else 80)
+            cut = P // 2 if len(parts) == 2 else (80 if e == E - 1 else 72)
             m = slice(0, cut) if q == 0 else slice(cut, P)
             raw = parts[q][:] if len(parts) == 2 else parts[0][:, :, PACK * m.start : PACK * m.stop]
             if (label, e) not in rounded:
@@ -127,7 +127,7 @@ def tile_moe_pkd_glu_relu_kernel(
                     nc.scalar.copy(view, src)
 
         def quarters(label, e):
-            return (slice(2, 4), slice(0, 2)) if (label, e) in tuple((a, b) for a in ("w1", "w3") for b in range(E)) else (slice(0, 4),)
+            return (slice(2, 4), slice(0, 2)) if (label, e) in (("w1", E - 1),) else (slice(0, 4),)
 
         def quant13(label, e):
             words = ring.tile([P, H], U32, name=f"words_{label}", align_bytes=64)
@@ -252,7 +252,7 @@ def tile_moe_pkd_glu_relu_kernel(
                         out=bank[:, (e - e0) * C : (e - e0 + 1) * C], lhsT=words[:, m].bitcast(FP8X4), lhsT_scale=scales[:, m],
                         rhs=h_codes[e][0][:].bitcast(FP8X4), rhs_scale=h_codes[e][1][:], start=True, stop=True,
                     )
-                if g in (() if b == 0 else ()):
+                if g in ((2,) if b == 0 else ()):
                     nc.vector.tensor_copy(y[:, e0 * C : e1 * C], bank[:, 0 : (e1 - e0) * C])
                 else:
                     nc.scalar.copy(y[:, e0 * C : e1 * C], bank[:, 0 : (e1 - e0) * C])

@@ -4,9 +4,9 @@ import concourse.mybir as mybir
 from concourse.masks import make_identity
 
 K, T, E, C, H, N = 512, 640, 5, 256, 512, 384
-S = E * C
-FLOPS = 2 * S * (2 * K * H + H * N)
-BYTES = 4 * E * (2 * K * H + H * N) + K * T + (K // 32) * T + 4 * 2 * T + 2 * (S + 2 * T) + 4 * N * T
+SLOTS = E * C
+FLOPS = 2 * SLOTS * (2 * K * H + H * N)
+BYTES = 4 * E * (2 * K * H + H * N) + K * T + (K // 32) * T + 4 * 2 * T + 2 * (SLOTS + 2 * T) + 4 * N * T
 
 F32 = mybir.dt.float32
 BF16 = mybir.dt.bfloat16
@@ -22,10 +22,12 @@ PACK = 4
 LIST = 16
 HALF = C // 2
 BLOCKS = N // P
-EARLY = 3
+LAST = E - 1
 GROUPS = ((0, 2), (2, 4), (4, 5))
-WHOLE = 0
-LAST_PIECES = (448,192,)
+SCALAR_W3 = 56
+SCALAR_W1 = 88
+SCALAR_W1_LAST = 80
+LAST_PIECES = (448, 192)
 
 
 def tile_moe_pkd_glu_relu_kernel(
@@ -35,268 +37,261 @@ def tile_moe_pkd_glu_relu_kernel(
     with ExitStack() as ctx:
         keep = ctx.enter_context(tc.tile_pool(name="keep", bufs=1))
         ring = ctx.enter_context(tc.tile_pool(name="ring", bufs=2))
-        low_ring = ctx.enter_context(tc.tile_pool(name="low_ring", bufs=2))
         psum = ctx.enter_context(tc.psum_pool(name="psum", bufs=1))
         psum_y = ctx.enter_context(tc.psum_pool(name="psum_y", bufs=4))
 
-        def held(shape, dtype, name, tag=None):
-            return keep.tile(shape, dtype, name=name, tag=tag or name, align_bytes=64)
+        def held(shape, dtype, name, over=None):
+            return keep.tile(shape, dtype, name=name, tag=over or name, align_bytes=64)
 
-        xw = held([P, T], I32, "xw")
-        xs = held([P, T], U8, "xs")
-        offs_t = keep.tile([P, S // LIST], U16, name="offs_t")
+        token_words = held([P, T], I32, "token_words")
+        token_scales = held([P, T], U8, "token_scales")
+        offs_t = keep.tile([P, SLOTS // LIST], U16, name="offs_t")
         pos1_t = keep.tile([P, T // LIST], U16, name="pos1_t")
         pos2_t = keep.tile([P, T // LIST], U16, name="pos2_t")
         gates = [held([P, T], F32, f"gate{r}") for r in range(2)]
-        nc.gpsimd.memset(xs[:].bitcast(I32), 0)
-        nc.sync.dma_start(out=xw[:], in_=x_words[0].rearrange("p t r -> p (t r)").bitcast(I32))
+        ident = held([P, P], F32, "ident")
+        nc.gpsimd.memset(token_scales[:].bitcast(I32), 0)
+        make_identity(nc, ident[:])
+        nc.sync.dma_start(out=token_words[:], in_=x_words[0].rearrange("p t r -> p (t r)").bitcast(I32))
         nc.sync.dma_start(out=offs_t[:], in_=offs)
 
-        ident = held([P, P], F32, "ident")
-        make_identity(nc, ident[:])
-        raw13 = {}
+        staged = {}
         for e in range(E):
             for label, w in (("w3", w3), ("w1", w1)):
-                parts = 2 if (label, e) in (("w3", 0), ) else 1
-                width = H // parts
-                raw13[label, e] = []
-                for q in range(parts):
-                    raw = held([P, PACK, width], F32, f"raw_{label}_{e}_{q}")
+                rows = w[e].rearrange("(p j) i -> p j i", j=PACK)
+                if (label, e) != ("w3", 0):
+                    staged[label, e] = held([P, PACK, H], F32, f"staged_{label}_{e}")
+                    nc.sync.dma_start(out=staged[label, e][:], in_=rows)
+                    continue
+                first_halves = [held([P, PACK, H // 2], F32, f"staged_w3_0_{q}") for q in range(2)]
+                nc.sync.dma_start(out=first_halves[0][:], in_=rows[:, :, 0 : H // 2])
+                for r in range(4):
                     nc.sync.dma_start(
-                        out=raw[:], in_=w[e, :, q * width : (q + 1) * width].rearrange("(p j) c -> p j c", j=PACK)
+                        out=token_scales[r:P:32, :].bitcast(I32), in_=x_scales[0, r:16:4, :].bitcast(I32)
                     )
-                    raw13[label, e].append(raw)
-                    if (label, e, q) == None:
-                        nc.sync.dma_start(out=pos1_t[:], in_=pos1)
-                        nc.sync.dma_start(out=gates[0][:], in_=gate[0, 0:P, :])
-                    if (label, e, q) == None:
-                        nc.sync.dma_start(out=pos2_t[:], in_=pos2)
-                        nc.sync.dma_start(out=gates[1][:], in_=gate[1, 0:P, :])
-                    if (label, e, q) == ("w3", 0, 0):
-                        for r in range(4):
-                            nc.sync.dma_start(out=xs[r:P:32, :].bitcast(I32), in_=x_scales[0, r:16:4, :].bitcast(I32))
-        raw2 = {}
+                nc.sync.dma_start(out=first_halves[1][:], in_=rows[:, :, H // 2 : H])
         for b in range(BLOCKS):
             for e0, e1 in GROUPS:
-                if e1 <= WHOLE:
-                    if b == 0:
-                        raw = held([P, e1 - e0, PACK, N], F32, f"raw_w2_{e0}")
-                        for e in range(e0, e1):
-                            nc.sync.dma_start(out=raw[:, e - e0], in_=w2[e].rearrange("(p j) n -> p j n", j=PACK))
-                        for c in range(BLOCKS):
-                            raw2[c, e0] = raw[:, :, :, c * P : (c + 1) * P]
-                    continue
-                raw = held([P, e1 - e0, PACK, P], F32, f"raw_w2_{b}_{e0}")
+                staged["w2", b, e0] = held([P, e1 - e0, PACK, P], F32, f"staged_w2_{b}_{e0}")
                 for e in range(e0, e1):
                     nc.sync.dma_start(
-                        out=raw[:, e - e0], in_=w2[e, :, b * P : (b + 1) * P].rearrange("(p j) n -> p j n", j=PACK)
+                        out=staged["w2", b, e0][:, e - e0],
+                        in_=w2[e, :, b * P : (b + 1) * P].rearrange("(p j) n -> p j n", j=PACK),
                     )
-                raw2[b, e0] = raw[:]
-            if b == 0 and None is None:
+            if b == 0:
                 nc.sync.dma_start(out=pos1_t[:], in_=pos1)
                 nc.sync.dma_start(out=gates[0][:], in_=gate[0, 0:P, :])
-            if b == 0 and None is None:
                 nc.sync.dma_start(out=pos2_t[:], in_=pos2)
                 nc.sync.dma_start(out=gates[1][:], in_=gate[1, 0:P, :])
 
-        xg_w, xg_s = {}, {}
+        slot_words, slot_scales = {}, {}
 
-        def gather_words(e, tag=None):
-            xg_w[e] = held([P, C], U32, f"xg_w{e}", tag)
-            nc.vector.tensor_copy(xg_w[e][:], xw[:].bitcast(U32).indirect(offs_t[:, e * C // LIST : (e + 1) * C // LIST]))
+        def gather_words(e, over=None):
+            slot_words[e] = held([P, C], U32, f"slot_words{e}", over)
+            entries = offs_t[:, e * C // LIST : (e + 1) * C // LIST]
+            nc.vector.tensor_copy(slot_words[e][:], token_words[:].bitcast(U32).indirect(entries))
 
-        def gather_scales(e, tag=None):
-            xg_s[e] = held([P, C], U8, f"xg_s{e}", tag)
-            nc.vector.tensor_copy(xg_s[e][:], xs[:].indirect(offs_t[:, e * C // LIST : (e + 1) * C // LIST]))
+        def gather_scales(e, over=None):
+            slot_scales[e] = held([P, C], U8, f"slot_scales{e}", over)
+            entries = offs_t[:, e * C // LIST : (e + 1) * C // LIST]
+            nc.vector.tensor_copy(slot_scales[e][:], token_scales[:].indirect(entries))
 
-        rounded, codes = {}, {}
+        rounded, codes, banks, up, h_rounded, h_codes = {}, {}, {}, {}, {}, {}
 
-        def round13(label, e, q, on_vector):
-            parts = raw13[label, e]
-            cut = P // 2 if len(parts) == 2 else (80 if e == E - 1 else 72)
-            m = slice(0, cut) if q == 0 else slice(cut, P)
-            raw = parts[q][:] if len(parts) == 2 else parts[0][:, :, PACK * m.start : PACK * m.stop]
-            if (label, e) not in rounded:
-                rounded[label, e] = low_ring.tile([P, PACK, P, PACK], BF16, name=f"bf_{label}", align_bytes=64)
-            for ts in quarters(label, e):
-                src = raw.rearrange("p j (m t) -> p m j t", t=PACK)[:, :, :, ts]
-                view = rounded[label, e][:, ts, m, :].rearrange("p t m j -> p m j t")
-                if on_vector:
-                    nc.vector.tensor_copy(view, src)
-                else:
-                    nc.scalar.copy(view, src)
+        def product_steps(label, e):
+            return (slice(2, 4), slice(0, 2)) if (label, e) == ("w1", LAST) else (slice(0, PACK),)
 
-        def quarters(label, e):
-            return (slice(2, 4), slice(0, 2)) if (label, e) in (("w1", E - 1),) else (slice(0, 4),)
+        def round_first(label, e):
+            rounded[label, e] = ring.tile([P, PACK, P, PACK], BF16, name=f"rounded_{label}", align_bytes=64)
+            target = rounded[label, e][:].rearrange("p t m j -> p m j t")
+            if (label, e) == ("w3", 0):
+                for q, half in enumerate(first_halves):
+                    source = half[:].rearrange("p j (m t) -> p m j t", t=PACK)
+                    nc.scalar.copy(target[:, q * P // 2 : (q + 1) * P // 2], source)
+                return
+            if label == "w3":
+                cut = SCALAR_W3
+            else:
+                cut = SCALAR_W1_LAST if e == LAST else SCALAR_W1
+            source = staged[label, e][:].rearrange("p j (m t) -> p m j t", t=PACK)
+            for ts in product_steps(label, e):
+                nc.scalar.copy(target[:, 0:cut, :, ts], source[:, 0:cut, :, ts])
+            for ts in product_steps(label, e):
+                nc.vector.tensor_copy(target[:, cut:P, :, ts], source[:, cut:P, :, ts])
 
-        def quant13(label, e):
+        def quantise_first(label, e):
             words = ring.tile([P, H], U32, name=f"words_{label}", align_bytes=64)
             scales = ring.tile([P, H], U8, name=f"scales_{label}", align_bytes=64)
-            for ts in quarters(label, e):
+            for ts in product_steps(label, e):
                 cols = slice(ts.start * P, ts.stop * P)
                 nc.vector.quantize_mx(
-                    out=words[:, cols].bitcast(FP8X4), scales=scales[:, cols],
+                    out=words[:, cols].bitcast(FP8X4),
+                    scales=scales[:, cols],
                     in_=rounded[label, e][:, ts].rearrange("p t m j -> p (t m j)"),
                 )
             codes[label, e] = (words, scales)
 
-        banks = {}
-
         def first_product(label, e):
+            pair = (e + (label == "w1")) % 2
             for s in range(2):
-                turn = (e + (label == "w1")) % 2
-                banks[label, e, s] = psum.tile([P, PACK, HALF], F32, name=f"bank_{label}", tag=f"bank{turn}_{s}")
+                banks[label, e, s] = psum.tile([P, PACK, HALF], F32, name=f"bank_{label}", tag=f"bank{pair}_{s}")
             words, scales = codes[label, e]
-            for ts in quarters(label, e):
+            for ts in product_steps(label, e):
                 for s in range(2):
-                    cols = slice(s * HALF, (s + 1) * HALF)
+                    slots = slice(s * HALF, (s + 1) * HALF)
                     for t in range(ts.start, ts.stop):
-                        m = slice(t * P, (t + 1) * P)
+                        cols = slice(t * P, (t + 1) * P)
                         nc.tensor.matmul_mx(
                             out=banks[label, e, s][:, t, :],
-                            lhsT=words[:, m].bitcast(FP8X4), lhsT_scale=scales[:, m],
-                            rhs=xg_w[e][:, cols].bitcast(FP8X4), rhs_scale=xg_s[e][:, cols], start=True, stop=True,
+                            lhsT=words[:, cols].bitcast(FP8X4),
+                            lhsT_scale=scales[:, cols],
+                            rhs=slot_words[e][:, slots].bitcast(FP8X4),
+                            rhs_scale=slot_scales[e][:, slots],
+                            start=True,
+                            stop=True,
                         )
-
-        up = {}
 
         def copy_up(e):
             for s in range(2):
-                up[e, s] = raw13["w1", e][0][:, 2 * s : 2 * s + 2, 0 : H // 2].rearrange("p r (c t) -> p r c t", t=PACK)
+                up[e, s] = staged["w1", e][:, 2 * s : 2 * s + 2, 0 : H // 2].rearrange("p r (c t) -> p r c t", t=PACK)
                 nc.scalar.copy(up[e, s], banks["w3", e, s][:].rearrange("p t (r c) -> p r c t", r=2))
-
-        h_bf, h_codes = {}, {}
 
         def hidden(e, s):
             if s == 0:
-                tag = f"raw_w3_{e + 1}_0" if e + 1 < E and e + 1 + EARLY >= E and False else None
-                h_bf[e] = held([P, 2, HALF, PACK], BF16, f"h_bf{e}", tag)
+                h_rounded[e] = held([P, 2, HALF, PACK], BF16, f"h_rounded{e}")
             nc.vector.scalar_tensor_tensor(
-                out=h_bf[e][:, s].rearrange("p (r c) t -> p r c t", r=2),
-                in0=banks["w1", e, s][:].rearrange("p t (r c) -> p r c t", r=2), scalar=0.0,
-                in1=up[e, s], op0=ALU.max, op1=ALU.mult,
+                out=h_rounded[e][:, s].rearrange("p (r c) t -> p r c t", r=2),
+                in0=banks["w1", e, s][:].rearrange("p t (r c) -> p r c t", r=2),
+                scalar=0.0,
+                in1=up[e, s],
+                op0=ALU.max,
+                op1=ALU.mult,
             )
 
-        def quant_h(e):
+        def quantise_hidden(e):
             words = held([P, C], U32, f"h_words{e}")
             scales = held([P, C], U8, f"h_scales{e}")
             nc.vector.quantize_mx(
-                out=words[:].bitcast(FP8X4), scales=scales[:], in_=h_bf[e][:].rearrange("p s c t -> p (s c t)")
+                out=words[:].bitcast(FP8X4), scales=scales[:], in_=h_rounded[e][:].rearrange("p s c t -> p (s c t)")
             )
             h_codes[e] = (words, scales)
 
-        for e in range(EARLY):
+        for e in range(LAST):
             gather_words(e)
-        for e in range(EARLY):
+        for e in range(LAST):
             gather_scales(e)
         for e in range(E):
-            round13("w3", e, 0, False)
-            round13("w3", e, 1, e not in (0,))
-            quant13("w3", e)
+            round_first("w3", e)
+            quantise_first("w3", e)
             if e >= 1:
                 hidden(e - 1, 0)
             first_product("w3", e)
-            round13("w1", e, 0, False)
-            round13("w1", e, 1, True)
+            round_first("w1", e)
             if e >= 1:
                 hidden(e - 1, 1)
             copy_up(e)
-            quant13("w1", e)
+            quantise_first("w1", e)
             if e >= 1:
-                quant_h(e - 1)
+                quantise_hidden(e - 1)
             first_product("w1", e)
-            if e + EARLY < E:
-                gather_words(e + EARLY, f"raw_w1_{e}_0")
-                gather_scales(e + EARLY, f"raw_w3_{e}_1" if e == 0 else f"raw_w3_{e}_0")
-        hidden(E - 1, 0)
-        hidden(E - 1, 1)
-        quant_h(E - 1)
-
-        w2_codes, w2_tag = {}, {}
+            if e == 0:
+                gather_words(LAST, over="staged_w1_0")
+                gather_scales(LAST, over="staged_w3_0_1")
+        hidden(LAST, 0)
+        hidden(LAST, 1)
+        quantise_hidden(LAST)
 
         def prepare_w2(b):
             words = held([P, E * P], U32, f"w2_words{b}")
             scales = held([P, E * P], U8, f"w2_scales{b}")
-            for g in ((0,1,2) if b == 0 else (0, 1, 2)):
-                e0, e1 = GROUPS[g]
-                tag = f"w2_words{b - 1}" if (b, g) in ((1, 0), ) else f"shared{b}_{g}"
-                if (b, g) == (0, 0) and None:
-                    tag = None
-                w2_tag[b, g] = tag
-                if (b, g) in ():
-                    dst = low_ring.tile([P, e1 - e0, P, PACK], BF16, name=f"w2_bf{b}_{g}", tag="bf_w1", align_bytes=64)
+            for g, (e0, e1) in enumerate(GROUPS):
+                over = "w2_words0" if (b, g) == (1, 0) else None
+                w2_rounded = held([P, e1 - e0, P, PACK], BF16, f"w2_rounded{b}_{g}", over)
+                target = w2_rounded[:].rearrange("p e (c i) j -> p e c j i", i=4)
+                source = staged["w2", b, e0][:].rearrange("p e j (c i) -> p e c j i", i=4)
+                if (b, g) == (0, 1):
+                    nc.vector.tensor_copy(target, source)
                 else:
-                    dst = held([P, e1 - e0, P, PACK], BF16, f"w2_bf{b}_{g}", tag)
-                view = dst[:].rearrange("p e (c i) j -> p e c j i", i=4)
-                src = raw2[b, e0].rearrange("p e j (c i) -> p e c j i", i=4)
-                if (b == 0 and g in (1,)) or (b, g) in ():
-                    nc.vector.tensor_copy(view, src)
-                else:
-                    nc.scalar.copy(view, src)
+                    nc.scalar.copy(target, source)
                 cols = slice(e0 * P, e1 * P)
                 nc.vector.quantize_mx(
-                    out=words[:, cols].bitcast(FP8X4), scales=scales[:, cols],
-                    in_=dst[:].rearrange("p e n j -> p (e n j)"),
+                    out=words[:, cols].bitcast(FP8X4),
+                    scales=scales[:, cols],
+                    in_=w2_rounded[:].rearrange("p e n j -> p (e n j)"),
                 )
-            w2_codes[b] = (words, scales)
+            return words, scales
 
-        def second_product(b):
-            y = held([P, S], F32, f"y{b}")
-            words, scales = w2_codes[b]
-            for g in ((0,1,2) if b == 0 else (0, 1, 2)):
-                e0, e1 = GROUPS[g]
+        def second_product(b, words, scales):
+            y = held([P, SLOTS], F32, f"y{b}")
+            for e0, e1 in GROUPS:
                 bank = psum_y.tile([P, 2 * C], F32, name="bank_y")
                 for e in range(e0, e1):
-                    m = slice(e * P, (e + 1) * P)
+                    cols = slice(e * P, (e + 1) * P)
                     nc.tensor.matmul_mx(
-                        out=bank[:, (e - e0) * C : (e - e0 + 1) * C], lhsT=words[:, m].bitcast(FP8X4), lhsT_scale=scales[:, m],
-                        rhs=h_codes[e][0][:].bitcast(FP8X4), rhs_scale=h_codes[e][1][:], start=True, stop=True,
+                        out=bank[:, (e - e0) * C : (e - e0 + 1) * C],
+                        lhsT=words[:, cols].bitcast(FP8X4),
+                        lhsT_scale=scales[:, cols],
+                        rhs=h_codes[e][0][:].bitcast(FP8X4),
+                        rhs_scale=h_codes[e][1][:],
+                        start=True,
+                        stop=True,
                     )
-                if g in ((2,) if b == 0 else ()):
+                if (b, e0) == (0, LAST):
                     nc.vector.tensor_copy(y[:, e0 * C : e1 * C], bank[:, 0 : (e1 - e0) * C])
                 else:
                     nc.scalar.copy(y[:, e0 * C : e1 * C], bank[:, 0 : (e1 - e0) * C])
             return y
 
-        def add_by_transposes(total, first, second):
+        def weighted_pair(b, y, t0, t1, over=None):
+            first = held([P, t1 - t0], F32, f"first{b}_{t0}")
+            second = held([P, t1 - t0], F32, f"second{b}_{t0}", over)
+            entries = slice(t0 // LIST, t1 // LIST)
+            nc.vector.tensor_tensor(first[:], y[:].indirect(pos1_t[:, entries]), gates[0][:, t0:t1], ALU.mult)
+            nc.vector.tensor_tensor(second[:], y[:].indirect(pos2_t[:, entries]), gates[1][:, t0:t1], ALU.mult)
+            return first, second
+
+        def add_on_vector(b, first, second, t0, t1, over=None):
+            total = held([P, t1 - t0], F32, f"total{b}_{t0}", over)
+            nc.vector.tensor_tensor(total[:], first[:], second[:], ALU.add)
+            nc.sync.dma_start(out=out[b * P : (b + 1) * P, t0:t1], in_=total[:])
+
+        def add_by_transposes(b, first, second):
+            total = held([P, T], F32, f"total{b}_0")
             turned = held([P, T], F32, "turned")
-            for c0, c1 in ((0, 3), (3, 5)):
-                bank = psum.tile([P, c1 - c0, P], F32, name="bank_turn", tag=f"bank0_{c0 // 3}")
+            runs = ((0, 3), (3, T // P))
+            for s, (c0, c1) in enumerate(runs):
+                bank = psum.tile([P, c1 - c0, P], F32, name="bank_turned", tag=f"bank0_{s}")
                 for c in range(c0, c1):
-                    for k, src in enumerate((first, second)):
+                    for term in (first, second):
                         nc.tensor.matmul(
-                            bank[:, c - c0, :], src[:, c * P : (c + 1) * P], ident[:],
-                            is_transpose=True, start=k == 0, stop=k == 1,
+                            bank[:, c - c0, :],
+                            term[:, c * P : (c + 1) * P],
+                            ident[:],
+                            is_transpose=True,
+                            start=term is first,
+                            stop=term is second,
                         )
                 nc.scalar.copy(turned[:, c0 * P : c1 * P], bank[:].rearrange("p c n -> p (c n)"))
-            for c0, c1 in ((0, 3), (3, 5)):
-                bank = psum.tile([P, c1 - c0, P], F32, name="bank_back", tag=f"bank1_{c0 // 3}")
+            for s, (c0, c1) in enumerate(runs):
+                bank = psum.tile([P, c1 - c0, P], F32, name="bank_back", tag=f"bank1_{s}")
                 for c in range(c0, c1):
                     nc.tensor.transpose(bank[:, c - c0, :], turned[:, c * P : (c + 1) * P], ident[:])
                 nc.scalar.copy(total[:, c0 * P : c1 * P], bank[:].rearrange("p c n -> p (c n)"))
+            nc.scalar.dma_start(out=out[b * P : (b + 1) * P, :], in_=total[:])
 
-        def combine(b, y, widths):
-            t0 = 0
-            for q, width in enumerate(widths):
-                tok = slice(t0, t0 + width)
-                lst = slice(t0 // LIST, (t0 + width) // LIST)
-                t0 = t0 + width
-                behind = b + 1 < BLOCKS
-                first = held([P, width], F32, f"first{b}_{q}")
-                second = held([P, width], F32, f"second{b}_{q}", w2_tag.get((b + 1, (1,2)[b])) if behind else None)
-                total = held([P, width], F32, f"total{b}_{q}", w2_tag.get((b + 1, (2,9)[b])) if behind else None)
-                nc.vector.tensor_tensor(first[:], y[:].indirect(pos1_t[:, lst]), gates[0][:, tok], ALU.mult)
-                nc.vector.tensor_tensor(second[:], y[:].indirect(pos2_t[:, lst]), gates[1][:, tok], ALU.mult)
-                if b == 1 and True:
-                    add_by_transposes(total, first, second)
-                else:
-                    nc.vector.tensor_tensor(total[:], first[:], second[:], ALU.add)
-                queue = nc.scalar if b == 1 and True else nc.sync
-                queue.dma_start(out=out[b * P : (b + 1) * P, tok], in_=total[:])
+        y = second_product(0, *prepare_w2(0))
+        w2_next = prepare_w2(1)
+        first, second = weighted_pair(0, y, 0, T, over="w2_rounded1_1")
+        add_on_vector(0, first, second, 0, T, over="w2_rounded1_2")
 
-        prepare_w2(0)
-        for b in range(BLOCKS):
-            y = second_product(b)
-            if b + 1 < BLOCKS:
-                prepare_w2(b + 1)
-            combine(b, y, LAST_PIECES if b == BLOCKS - 1 else (T,))
+        y = second_product(1, *w2_next)
+        w2_next = prepare_w2(2)
+        first, second = weighted_pair(1, y, 0, T, over="w2_rounded2_2")
+        add_by_transposes(1, first, second)
+
+        y = second_product(2, *w2_next)
+        t0 = 0
+        for width in LAST_PIECES:
+            first, second = weighted_pair(2, y, t0, t0 + width)
+            add_on_vector(2, first, second, t0, t0 + width)
+            t0 = t0 + width

@@ -23,10 +23,11 @@ LIST = 16
 HALF = C // 2
 BLOCKS = N // P
 LAST = E - 1
+WINDOW = 704
 GROUPS = ((0, 2), (2, 4), (4, 5))
-SCALAR_W3 = 56
+SCALAR_W3 = 64
 SCALAR_W1 = 88
-SCALAR_W1_LAST = 80
+SCALAR_W1_LAST = 64
 LAST_PIECES = (448, 192)
 
 
@@ -38,21 +39,21 @@ def tile_moe_pkd_glu_relu_kernel(
         keep = ctx.enter_context(tc.tile_pool(name="keep", bufs=1))
         ring = ctx.enter_context(tc.tile_pool(name="ring", bufs=2))
         psum = ctx.enter_context(tc.psum_pool(name="psum", bufs=1))
-        psum_y = ctx.enter_context(tc.psum_pool(name="psum_y", bufs=4))
 
         def held(shape, dtype, name, over=None):
             return keep.tile(shape, dtype, name=name, tag=over or name, align_bytes=64)
 
-        token_words = held([P, T], I32, "token_words")
-        token_scales = held([P, T], U8, "token_scales")
+        token_words = held([P, WINDOW], I32, "token_words")
+        token_scales = held([P, WINDOW], U8, "token_scales")
         offs_t = keep.tile([P, SLOTS // LIST], U16, name="offs_t")
         pos1_t = keep.tile([P, T // LIST], U16, name="pos1_t")
         pos2_t = keep.tile([P, T // LIST], U16, name="pos2_t")
         gates = [held([P, T], F32, f"gate{r}") for r in range(2)]
         ident = held([P, P], F32, "ident")
         nc.gpsimd.memset(token_scales[:].bitcast(I32), 0)
+        nc.gpsimd.memset(token_words[:, T:WINDOW], 0)
         make_identity(nc, ident[:])
-        nc.sync.dma_start(out=token_words[:], in_=x_words[0].rearrange("p t r -> p (t r)").bitcast(I32))
+        nc.sync.dma_start(out=token_words[:, 0:T], in_=x_words[0].rearrange("p t r -> p (t r)").bitcast(I32))
         nc.sync.dma_start(out=offs_t[:], in_=offs)
 
         staged = {}
@@ -67,7 +68,7 @@ def tile_moe_pkd_glu_relu_kernel(
                 nc.sync.dma_start(out=first_halves[0][:], in_=rows[:, :, 0 : H // 2])
                 for r in range(4):
                     nc.sync.dma_start(
-                        out=token_scales[r:P:32, :].bitcast(I32), in_=x_scales[0, r:16:4, :].bitcast(I32)
+                        out=token_scales[r:P:32, 0:T].bitcast(I32), in_=x_scales[0, r:16:4, :].bitcast(I32)
                     )
                 nc.sync.dma_start(out=first_halves[1][:], in_=rows[:, :, H // 2 : H])
         for b in range(BLOCKS):
@@ -78,23 +79,23 @@ def tile_moe_pkd_glu_relu_kernel(
                         out=staged["w2", b, e0][:, e - e0],
                         in_=w2[e, :, b * P : (b + 1) * P].rearrange("(p j) n -> p j n", j=PACK),
                     )
-            if b == 0:
-                nc.sync.dma_start(out=pos1_t[:], in_=pos1)
-                nc.sync.dma_start(out=gates[0][:], in_=gate[0, 0:P, :])
-                nc.sync.dma_start(out=pos2_t[:], in_=pos2)
-                nc.sync.dma_start(out=gates[1][:], in_=gate[1, 0:P, :])
+            if b < 2:
+                nc.sync.dma_start(out=(pos1_t, pos2_t)[b][:], in_=(pos1, pos2)[b])
+                nc.sync.dma_start(out=gates[b][:], in_=gate[b, 0:P, :])
 
         slot_words, slot_scales = {}, {}
 
-        def gather_words(e, over=None):
-            slot_words[e] = held([P, C], U32, f"slot_words{e}", over)
-            entries = offs_t[:, e * C // LIST : (e + 1) * C // LIST]
-            nc.vector.tensor_copy(slot_words[e][:], token_words[:].bitcast(U32).indirect(entries))
+        def gather(window, dtype, into, label, e0, e1, over=None):
+            tile = held([P, (e1 - e0) * C], dtype, f"slot_{label}{e0}", over)
+            nc.vector.tensor_copy(tile[:], window.indirect(offs_t[:, e0 * C // LIST : e1 * C // LIST]))
+            for e in range(e0, e1):
+                into[e] = tile[:, (e - e0) * C : (e - e0 + 1) * C]
 
-        def gather_scales(e, over=None):
-            slot_scales[e] = held([P, C], U8, f"slot_scales{e}", over)
-            entries = offs_t[:, e * C // LIST : (e + 1) * C // LIST]
-            nc.vector.tensor_copy(slot_scales[e][:], token_scales[:].indirect(entries))
+        def gather_words(e0, e1, over=None):
+            gather(token_words[:].bitcast(U32), U32, slot_words, "words", e0, e1, over)
+
+        def gather_scales(e0, e1, over=None):
+            gather(token_scales[:], U8, slot_scales, "scales", e0, e1, over)
 
         rounded, codes, banks, up, h_rounded, h_codes = {}, {}, {}, {}, {}, {}
 
@@ -109,11 +110,14 @@ def tile_moe_pkd_glu_relu_kernel(
                     source = half[:].rearrange("p j (m t) -> p m j t", t=PACK)
                     nc.scalar.copy(target[:, q * P // 2 : (q + 1) * P // 2], source)
                 return
+            source = staged[label, e][:].rearrange("p j (m t) -> p m j t", t=PACK)
+            if e == 0:
+                nc.scalar.copy(target, source)
+                return
             if label == "w3":
                 cut = SCALAR_W3
             else:
                 cut = SCALAR_W1_LAST if e == LAST else SCALAR_W1
-            source = staged[label, e][:].rearrange("p j (m t) -> p m j t", t=PACK)
             for ts in product_steps(label, e):
                 nc.scalar.copy(target[:, 0:cut, :, ts], source[:, 0:cut, :, ts])
             for ts in product_steps(label, e):
@@ -132,9 +136,8 @@ def tile_moe_pkd_glu_relu_kernel(
             codes[label, e] = (words, scales)
 
         def first_product(label, e):
-            pair = (e + (label == "w1")) % 2
             for s in range(2):
-                banks[label, e, s] = psum.tile([P, PACK, HALF], F32, name=f"bank_{label}", tag=f"bank{pair}_{s}")
+                banks[label, e, s] = psum.tile([P, PACK, HALF], F32, name=f"bank_{label}", tag=f"{label}_{e % 2}_{s}")
             words, scales = codes[label, e]
             for ts in product_steps(label, e):
                 for s in range(2):
@@ -152,16 +155,17 @@ def tile_moe_pkd_glu_relu_kernel(
                         )
 
         def copy_up(e):
+            host = staged["w1", e]
             for s in range(2):
-                up[e, s] = staged["w1", e][:, 2 * s : 2 * s + 2, 0 : H // 2].rearrange("p r (c t) -> p r c t", t=PACK)
-                nc.scalar.copy(up[e, s], banks["w3", e, s][:].rearrange("p t (r c) -> p r c t", r=2))
+                up[e, s] = host[:, :, s * P : (s + 1) * P].rearrange("p r (c t) -> p r c t", t=PACK)
+                nc.scalar.copy(up[e, s], banks["w3", e, s][:].rearrange("p t (r c) -> p r c t", r=PACK))
 
         def hidden(e, s):
             if s == 0:
                 h_rounded[e] = held([P, 2, HALF, PACK], BF16, f"h_rounded{e}")
             nc.vector.scalar_tensor_tensor(
-                out=h_rounded[e][:, s].rearrange("p (r c) t -> p r c t", r=2),
-                in0=banks["w1", e, s][:].rearrange("p t (r c) -> p r c t", r=2),
+                out=h_rounded[e][:, s].rearrange("p (r c) t -> p r c t", r=PACK),
+                in0=banks["w1", e, s][:].rearrange("p t (r c) -> p r c t", r=PACK),
                 scalar=0.0,
                 in1=up[e, s],
                 op0=ALU.max,
@@ -176,10 +180,10 @@ def tile_moe_pkd_glu_relu_kernel(
             )
             h_codes[e] = (words, scales)
 
-        for e in range(LAST):
-            gather_words(e)
-        for e in range(LAST):
-            gather_scales(e)
+        for e0, e1 in GROUPS[:-1]:
+            gather_words(e0, e1)
+        for e0, e1 in GROUPS[:-1]:
+            gather_scales(e0, e1)
         for e in range(E):
             round_first("w3", e)
             quantise_first("w3", e)
@@ -195,8 +199,8 @@ def tile_moe_pkd_glu_relu_kernel(
                 quantise_hidden(e - 1)
             first_product("w1", e)
             if e == 0:
-                gather_words(LAST, over="staged_w1_0")
-                gather_scales(LAST, over="staged_w3_0_1")
+                gather_words(LAST, E, over="staged_w3_0_0")
+                gather_scales(LAST, E, over="staged_w3_0_1")
         hidden(LAST, 0)
         hidden(LAST, 1)
         quantise_hidden(LAST)
@@ -205,14 +209,16 @@ def tile_moe_pkd_glu_relu_kernel(
             words = held([P, E * P], U32, f"w2_words{b}")
             scales = held([P, E * P], U8, f"w2_scales{b}")
             for g, (e0, e1) in enumerate(GROUPS):
-                over = "w2_words0" if (b, g) == (1, 0) else None
-                w2_rounded = held([P, e1 - e0, P, PACK], BF16, f"w2_rounded{b}_{g}", over)
+                w2_rounded = held([P, e1 - e0, P, PACK], BF16, f"w2_rounded{b}_{g}")
                 target = w2_rounded[:].rearrange("p e (c i) j -> p e c j i", i=4)
                 source = staged["w2", b, e0][:].rearrange("p e j (c i) -> p e c j i", i=4)
-                if (b, g) == (0, 1):
+                if g == 2 or (b, g) == (0, 0):
                     nc.vector.tensor_copy(target, source)
-                else:
+                elif g == 0:
                     nc.scalar.copy(target, source)
+                else:
+                    for q in range(e1 - e0):
+                        nc.scalar.copy(target[:, q], source[:, q])
                 cols = slice(e0 * P, e1 * P)
                 nc.vector.quantize_mx(
                     out=words[:, cols].bitcast(FP8X4),
@@ -222,9 +228,10 @@ def tile_moe_pkd_glu_relu_kernel(
             return words, scales
 
         def second_product(b, words, scales):
-            y = held([P, SLOTS], F32, f"y{b}")
-            for e0, e1 in GROUPS:
-                bank = psum_y.tile([P, 2 * C], F32, name="bank_y")
+            y = held([P, SLOTS], F32, f"y{b}", f"staged_w2_{b}_2" if b > 0 else None)
+            for g, (e0, e1) in enumerate(GROUPS):
+                turn = (b * len(GROUPS) + g) % 4
+                bank = psum.tile([P, 2 * C], F32, name="bank_y", tag=f"{('w3', 'w1')[turn // 2]}_1_{turn % 2}")
                 for e in range(e0, e1):
                     cols = slice(e * P, (e + 1) * P)
                     nc.tensor.matmul_mx(
@@ -257,10 +264,10 @@ def tile_moe_pkd_glu_relu_kernel(
 
         def add_by_transposes(b, first, second):
             total = held([P, T], F32, f"total{b}_0")
-            turned = held([P, T], F32, "turned")
+            turned = held([P, T], F32, "turned", "w2_words2")
             runs = ((0, 3), (3, T // P))
             for s, (c0, c1) in enumerate(runs):
-                bank = psum.tile([P, c1 - c0, P], F32, name="bank_turned", tag=f"bank0_{s}")
+                bank = psum.tile([P, c1 - c0, P], F32, name="bank_turned", tag=f"w3_0_{s}")
                 for c in range(c0, c1):
                     for term in (first, second):
                         nc.tensor.matmul(
@@ -273,7 +280,7 @@ def tile_moe_pkd_glu_relu_kernel(
                         )
                 nc.scalar.copy(turned[:, c0 * P : c1 * P], bank[:].rearrange("p c n -> p (c n)"))
             for s, (c0, c1) in enumerate(runs):
-                bank = psum.tile([P, c1 - c0, P], F32, name="bank_back", tag=f"bank1_{s}")
+                bank = psum.tile([P, c1 - c0, P], F32, name="bank_back", tag=f"w1_0_{s}")
                 for c in range(c0, c1):
                     nc.tensor.transpose(bank[:, c - c0, :], turned[:, c * P : (c + 1) * P], ident[:])
                 nc.scalar.copy(total[:, c0 * P : c1 * P], bank[:].rearrange("p c n -> p (c n)"))
@@ -281,15 +288,13 @@ def tile_moe_pkd_glu_relu_kernel(
 
         y = second_product(0, *prepare_w2(0))
         w2_next = prepare_w2(1)
-        first, second = weighted_pair(0, y, 0, T, over="w2_rounded1_1")
-        add_on_vector(0, first, second, 0, T, over="w2_rounded1_2")
-
+        pair0 = weighted_pair(0, y, 0, T, over="w2_rounded1_1")
         y = second_product(1, *w2_next)
         w2_next = prepare_w2(2)
-        first, second = weighted_pair(1, y, 0, T, over="w2_rounded2_2")
-        add_by_transposes(1, first, second)
-
+        pair1 = weighted_pair(1, y, 0, T, over="w2_rounded2_1")
+        add_on_vector(1, *pair1, 0, T)
         y = second_product(2, *w2_next)
+        add_by_transposes(0, *pair0)
         t0 = 0
         for width in LAST_PIECES:
             first, second = weighted_pair(2, y, t0, t0 + width)

@@ -27,7 +27,7 @@ WINDOW = 704
 GROUPS = ((0, 2), (2, 4), (4, 5))
 SCALAR_W3 = 64
 SCALAR_W1 = 88
-SCALAR_W1_LAST = 64
+SCALAR_W1_LAST = 48
 LAST_PIECES = (448, 192)
 
 
@@ -212,9 +212,9 @@ def tile_moe_pkd_glu_relu_kernel(
                 w2_rounded = held([P, e1 - e0, P, PACK], BF16, f"w2_rounded{b}_{g}")
                 target = w2_rounded[:].rearrange("p e (c i) j -> p e c j i", i=4)
                 source = staged["w2", b, e0][:].rearrange("p e j (c i) -> p e c j i", i=4)
-                if g == 2 or (b, g) == (0, 0):
+                if g == (0 if b == 0 else 2):
                     nc.vector.tensor_copy(target, source)
-                elif g == 0:
+                elif g != 1:
                     nc.scalar.copy(target, source)
                 else:
                     for q in range(e1 - e0):
@@ -228,7 +228,7 @@ def tile_moe_pkd_glu_relu_kernel(
             return words, scales
 
         def second_product(b, words, scales):
-            y = held([P, SLOTS], F32, f"y{b}", f"staged_w2_{b}_2" if b > 0 else None)
+            y = held([P, SLOTS], F32, f"y{b}", f"staged_w2_{b}_{2 if b > 0 else LAST}")
             for g, (e0, e1) in enumerate(GROUPS):
                 turn = (b * len(GROUPS) + g) % 4
                 bank = psum.tile([P, 2 * C], F32, name="bank_y", tag=f"{('w3', 'w1')[turn // 2]}_1_{turn % 2}")

@@ -71,17 +71,22 @@ def tile_moe_pkd_glu_relu_kernel(
                         out=token_scales[r:P:32, 0:T].bitcast(I32), in_=x_scales[0, r:16:4, :].bitcast(I32)
                     )
                 nc.sync.dma_start(out=first_halves[1][:], in_=rows[:, :, H // 2 : H])
-        for b in range(BLOCKS):
-            for e0, e1 in GROUPS:
-                staged["w2", b, e0] = held([P, e1 - e0, PACK, P], F32, f"staged_w2_{b}_{e0}")
-                for e in range(e0, e1):
-                    nc.sync.dma_start(
-                        out=staged["w2", b, e0][:, e - e0],
-                        in_=w2[e, :, b * P : (b + 1) * P].rearrange("(p j) n -> p j n", j=PACK),
-                    )
-            if b < 2:
-                nc.sync.dma_start(out=(pos1_t, pos2_t)[b][:], in_=(pos1, pos2)[b])
-                nc.sync.dma_start(out=gates[b][:], in_=gate[b, 0:P, :])
+        def load_w2(e, b0, b1):
+            tile = held([P, PACK, (b1 - b0) * P], F32, f"staged_w2_{e}_{b0}")
+            nc.sync.dma_start(out=tile[:], in_=w2[e, :, b0 * P : b1 * P].rearrange("(p j) n -> p j n", j=PACK))
+            for b in range(b0, b1):
+                staged["w2", b, e] = tile[:, :, (b - b0) * P : (b - b0 + 1) * P]
+
+        def load_gate(r):
+            nc.sync.dma_start(out=(pos1_t, pos2_t)[r][:], in_=(pos1, pos2)[r])
+            nc.sync.dma_start(out=gates[r][:], in_=gate[r, 0:P, :])
+
+        for e in range(E):
+            load_w2(e, 0, 2)
+        load_gate(0)
+        load_gate(1)
+        for e in range(E):
+            load_w2(e, 2, 3)
 
         slot_words, slot_scales = {}, {}
 
@@ -201,65 +206,69 @@ def tile_moe_pkd_glu_relu_kernel(
             if e == 0:
                 gather_words(LAST, E, over="staged_w3_0_0")
                 gather_scales(LAST, E, over="staged_w3_0_1")
-        hidden(LAST, 0)
-        hidden(LAST, 1)
-        quantise_hidden(LAST)
 
-        def prepare_w2(b):
-            words = held([P, E * P], U32, f"w2_words{b}")
-            scales = held([P, E * P], U8, f"w2_scales{b}")
-            for g, (e0, e1) in enumerate(GROUPS):
-                w2_rounded = held([P, e1 - e0, P, PACK], BF16, f"w2_rounded{b}_{g}")
-                target = w2_rounded[:].rearrange("p e (c i) j -> p e c j i", i=4)
-                source = staged["w2", b, e0][:].rearrange("p e j (c i) -> p e c j i", i=4)
-                if g == (0 if b == 0 else 2):
-                    nc.vector.tensor_copy(target, source)
-                elif g != 1:
-                    nc.scalar.copy(target, source)
-                else:
-                    for q in range(e1 - e0):
-                        nc.scalar.copy(target[:, q], source[:, q])
-                cols = slice(e0 * P, e1 * P)
-                nc.vector.quantize_mx(
-                    out=words[:, cols].bitcast(FP8X4),
-                    scales=scales[:, cols],
-                    in_=w2_rounded[:].rearrange("p e n j -> p (e n j)"),
-                )
-            return words, scales
+        w2_rounded, w2_codes, y, y_banks = {}, {}, {}, {}
+        BANK = {0: ("w3_1_0", "w3_1_1", "w1_1_0"), 1: ("w1_1_1", "w3_0_0", "w3_0_1"), 2: ("w3_1_0", "w3_1_1", "w1_1_0")}
 
-        def second_product(b, words, scales):
-            y = held([P, SLOTS], F32, f"y{b}", f"staged_w2_{b}_{2 if b > 0 else LAST}")
-            for g, (e0, e1) in enumerate(GROUPS):
-                turn = (b * len(GROUPS) + g) % 4
-                bank = psum.tile([P, 2 * C], F32, name="bank_y", tag=f"{('w3', 'w1')[turn // 2]}_1_{turn % 2}")
-                for e in range(e0, e1):
-                    cols = slice(e * P, (e + 1) * P)
-                    nc.tensor.matmul_mx(
-                        out=bank[:, (e - e0) * C : (e - e0 + 1) * C],
-                        lhsT=words[:, cols].bitcast(FP8X4),
-                        lhsT_scale=scales[:, cols],
-                        rhs=h_codes[e][0][:].bitcast(FP8X4),
-                        rhs_scale=h_codes[e][1][:],
-                        start=True,
-                        stop=True,
-                    )
-                if (b, e0) == (0, LAST):
-                    nc.vector.tensor_copy(y[:, e0 * C : e1 * C], bank[:, 0 : (e1 - e0) * C])
-                else:
-                    nc.scalar.copy(y[:, e0 * C : e1 * C], bank[:, 0 : (e1 - e0) * C])
-            return y
+        SPANS = {0: GROUPS, 1: ((0, 4), (4, 5)), 2: GROUPS}
 
-        def weighted_pair(b, y, t0, t1, over=None):
-            first = held([P, t1 - t0], F32, f"first{b}_{t0}")
-            second = held([P, t1 - t0], F32, f"second{b}_{t0}", over)
+        def round_w2(b, e, engine):
+            e0, e1 = [span for span in SPANS[b] if span[0] <= e < span[1]][0]
+            if e == e0:
+                w2_rounded[b, e0] = held([P, e1 - e0, P, PACK], BF16, f"w2_rounded{b}_{e}")
+            target = w2_rounded[b, e0][:, e - e0].rearrange("p (c i) j -> p c j i", i=4)
+            source = staged["w2", b, e].rearrange("p j (c i) -> p c j i", i=4)
+            if engine == "vector":
+                nc.vector.tensor_copy(target, source)
+            else:
+                nc.scalar.copy(target, source)
+
+        def quantise_w2(b, e, e1):
+            if e == 0:
+                over = "w2_rounded0_4" if b == 1 else None
+                w2_codes[b] = (held([P, E * P], U32, f"w2_words{b}", over), held([P, E * P], U8, f"w2_scales{b}"))
+            words, scales = w2_codes[b]
+            cols = slice(e * P, e1 * P)
+            nc.vector.quantize_mx(
+                out=words[:, cols].bitcast(FP8X4),
+                scales=scales[:, cols],
+                in_=w2_rounded[b, e][:].rearrange("p e n j -> p (e n j)"),
+            )
+
+        def second_product(b, e):
+            g = e // 2
+            if e % 2 == 0:
+                y_banks[b, g] = psum.tile([P, 2 * C], F32, name="bank_y", tag=BANK[b][g])
+            words, scales = w2_codes[b]
+            cols = slice(e * P, (e + 1) * P)
+            nc.tensor.matmul_mx(
+                out=y_banks[b, g][:, (e % 2) * C : (e % 2 + 1) * C],
+                lhsT=words[:, cols].bitcast(FP8X4),
+                lhsT_scale=scales[:, cols],
+                rhs=h_codes[e][0][:].bitcast(FP8X4),
+                rhs_scale=h_codes[e][1][:],
+                start=True,
+                stop=True,
+            )
+
+        def copy_y(b, g, engine="scalar"):
+            if g == 0:
+                y[b] = held([P, SLOTS], F32, f"y{b}", {0: "staged_w2_3_0", 2: "staged_w2_4_2"}.get(b))
+            e0, e1 = GROUPS[g]
+            if engine == "vector":
+                nc.vector.tensor_copy(y[b][:, e0 * C : e1 * C], y_banks[b, g][:, 0 : (e1 - e0) * C])
+            else:
+                nc.scalar.copy(y[b][:, e0 * C : e1 * C], y_banks[b, g][:, 0 : (e1 - e0) * C])
+
+        def weighted(b, r, t0, t1, over=None):
+            term = held([P, t1 - t0], F32, f"term{b}_{r}_{t0}", over)
             entries = slice(t0 // LIST, t1 // LIST)
-            nc.vector.tensor_tensor(first[:], y[:].indirect(pos1_t[:, entries]), gates[0][:, t0:t1], ALU.mult)
-            nc.vector.tensor_tensor(second[:], y[:].indirect(pos2_t[:, entries]), gates[1][:, t0:t1], ALU.mult)
-            return first, second
+            nc.vector.tensor_tensor(term[:], y[b][:].indirect((pos1_t, pos2_t)[r][:, entries]), gates[r][:, t0:t1], ALU.mult)
+            return term
 
         def add_on_vector(b, first, second, t0, t1, over=None):
             total = held([P, t1 - t0], F32, f"total{b}_{t0}", over)
-            nc.vector.tensor_tensor(total[:], first[:], second[:], ALU.add)
+            nc.vector.tensor_tensor(total[:], first, second, ALU.add)
             nc.sync.dma_start(out=out[b * P : (b + 1) * P, t0:t1], in_=total[:])
 
         def add_by_transposes(b, first, second):
@@ -267,7 +276,7 @@ def tile_moe_pkd_glu_relu_kernel(
             turned = held([P, T], F32, "turned", "w2_words2")
             runs = ((0, 3), (3, T // P))
             for s, (c0, c1) in enumerate(runs):
-                bank = psum.tile([P, c1 - c0, P], F32, name="bank_turned", tag=f"w3_0_{s}")
+                bank = psum.tile([P, c1 - c0, P], F32, name="bank_turned", tag=f"w1_0_{s}")
                 for c in range(c0, c1):
                     for term in (first, second):
                         nc.tensor.matmul(
@@ -280,23 +289,56 @@ def tile_moe_pkd_glu_relu_kernel(
                         )
                 nc.scalar.copy(turned[:, c0 * P : c1 * P], bank[:].rearrange("p c n -> p (c n)"))
             for s, (c0, c1) in enumerate(runs):
-                bank = psum.tile([P, c1 - c0, P], F32, name="bank_back", tag=f"w1_0_{s}")
+                bank = psum.tile([P, c1 - c0, P], F32, name="bank_back", tag=("w1_1_1", "w3_0_0")[s])
                 for c in range(c0, c1):
                     nc.tensor.transpose(bank[:, c - c0, :], turned[:, c * P : (c + 1) * P], ident[:])
                 nc.scalar.copy(total[:, c0 * P : c1 * P], bank[:].rearrange("p c n -> p (c n)"))
             nc.scalar.dma_start(out=out[b * P : (b + 1) * P, :], in_=total[:])
 
-        y = second_product(0, *prepare_w2(0))
-        w2_next = prepare_w2(1)
-        pair0 = weighted_pair(0, y, 0, T, over="w2_rounded1_1")
-        y = second_product(1, *w2_next)
-        w2_next = prepare_w2(2)
-        pair1 = weighted_pair(1, y, 0, T, over="w2_rounded2_1")
-        add_on_vector(1, *pair1, 0, T)
-        y = second_product(2, *w2_next)
-        add_by_transposes(0, *pair0)
-        t0 = 0
-        for width in LAST_PIECES:
-            first, second = weighted_pair(2, y, t0, t0 + width)
-            add_on_vector(2, first, second, t0, t0 + width)
-            t0 = t0 + width
+        def qm(b, g):
+            e0, e1 = SPANS[b][g]
+            quantise_w2(b, e0, e1)
+            for e in range(e0, e1):
+                second_product(b, e)
+
+        round_w2(0, 0, "vector")
+        hidden(LAST, 0)
+        hidden(LAST, 1)
+        round_w2(0, 1, "vector")
+        quantise_hidden(LAST)
+        qm(0, 0)
+        for e in range(E):
+            round_w2(1, e, "scalar")
+        round_w2(0, 2, "vector")
+        round_w2(0, 3, "vector")
+        qm(0, 1)
+        round_w2(0, 4, "vector")
+        qm(0, 2)
+        qm(1, 0)
+        qm(1, 1)
+        copy_y(0, 0)
+        copy_y(0, 1)
+        copy_y(0, 2, "vector")
+        first0 = weighted(0, 0, 0, T)
+        copy_y(1, 0)
+        copy_y(1, 1)
+        copy_y(1, 2)
+        second0 = weighted(0, 1, 0, T)
+        for e in range(E):
+            round_w2(2, e, "scalar")
+        first1 = weighted(1, 0, 0, T)
+        qm(2, 0)
+        qm(2, 1)
+        qm(2, 2)
+        second1 = weighted(1, 1, 0, T, "w2_rounded2_4")
+        for g in range(3):
+            copy_y(2, g)
+        add_by_transposes(0, first0, second0)
+        add_on_vector(1, first1[:], second1[:], 0, T)
+        first2 = weighted(2, 0, 0, T)
+        cuts = (0, 320, 512, T)
+        second2 = [weighted(2, 1, cuts[0], cuts[1]), weighted(2, 1, cuts[1], cuts[2])]
+        add_on_vector(2, first2[:, cuts[0] : cuts[1]], second2[0][:], cuts[0], cuts[1])
+        second2.append(weighted(2, 1, cuts[2], cuts[3]))
+        add_on_vector(2, first2[:, cuts[1] : cuts[2]], second2[1][:], cuts[1], cuts[2])
+        add_on_vector(2, first2[:, cuts[2] : cuts[3]], second2[2][:], cuts[2], cuts[3])

@@ -28,7 +28,8 @@ GROUPS = ((0, 2), (2, 4), (4, 5))
 SCALAR_W3 = 64
 SCALAR_W1 = 88
 SCALAR_W1_LAST = 48
-LAST_PIECES = (448, 192)
+LAST_CUTS = (0, 320, 512, T)
+Y_BANKS = (("w3_1_0", "w3_1_1", "w1_1_0"), ("w1_1_1", "w3_0_0", "w3_0_1"), ("w3_1_0", "w3_1_1", "w1_1_0"))
 
 
 def tile_moe_pkd_glu_relu_kernel(
@@ -71,22 +72,24 @@ def tile_moe_pkd_glu_relu_kernel(
                         out=token_scales[r:P:32, 0:T].bitcast(I32), in_=x_scales[0, r:16:4, :].bitcast(I32)
                     )
                 nc.sync.dma_start(out=first_halves[1][:], in_=rows[:, :, H // 2 : H])
-        def load_w2(e, b0, b1):
-            tile = held([P, PACK, (b1 - b0) * P], F32, f"staged_w2_{e}_{b0}")
-            nc.sync.dma_start(out=tile[:], in_=w2[e, :, b0 * P : b1 * P].rearrange("(p j) n -> p j n", j=PACK))
-            for b in range(b0, b1):
-                staged["w2", b, e] = tile[:, :, (b - b0) * P : (b - b0 + 1) * P]
+
+        def load_w2(b, e):
+            staged["w2", b, e] = held([P, PACK, P], F32, f"staged_w2_{b}_{e}")
+            nc.sync.dma_start(
+                out=staged["w2", b, e][:], in_=w2[e, :, b * P : (b + 1) * P].rearrange("(p j) n -> p j n", j=PACK)
+            )
 
         def load_gate(r):
             nc.sync.dma_start(out=(pos1_t, pos2_t)[r][:], in_=(pos1, pos2)[r])
             nc.sync.dma_start(out=gates[r][:], in_=gate[r, 0:P, :])
 
-        for e in range(E):
-            load_w2(e, 0, 2)
-        load_gate(0)
-        load_gate(1)
-        for e in range(E):
-            load_w2(e, 2, 3)
+        for b in range(BLOCKS):
+            for e in range(E):
+                load_w2(b, e)
+                if (b, e) == (1, 1):
+                    load_gate(0)
+            if b == 1:
+                load_gate(1)
 
         slot_words, slot_scales = {}, {}
 
@@ -208,66 +211,52 @@ def tile_moe_pkd_glu_relu_kernel(
                 gather_scales(LAST, E, over="staged_w3_0_1")
 
         w2_rounded, w2_codes, y, y_banks = {}, {}, {}, {}
-        BANK = {0: ("w3_1_0", "w3_1_1", "w1_1_0"), 1: ("w1_1_1", "w3_0_0", "w3_0_1"), 2: ("w3_1_0", "w3_1_1", "w1_1_0")}
+        on_vector, on_scalar = nc.vector.tensor_copy, nc.scalar.copy
 
-        SPANS = {0: GROUPS, 1: ((0, 4), (4, 5)), 2: GROUPS}
-
-        def round_w2(b, e, engine):
-            e0, e1 = [span for span in SPANS[b] if span[0] <= e < span[1]][0]
+        def round_w2(b, e, copy):
+            e0, e1 = GROUPS[e // 2]
             if e == e0:
-                w2_rounded[b, e0] = held([P, e1 - e0, P, PACK], BF16, f"w2_rounded{b}_{e}")
+                w2_rounded[b, e0] = held([P, e1 - e0, P, PACK], BF16, f"w2_rounded{b}_{e0}")
             target = w2_rounded[b, e0][:, e - e0].rearrange("p (c i) j -> p c j i", i=4)
-            source = staged["w2", b, e].rearrange("p j (c i) -> p c j i", i=4)
-            if engine == "vector":
-                nc.vector.tensor_copy(target, source)
-            else:
-                nc.scalar.copy(target, source)
+            copy(target, staged["w2", b, e][:].rearrange("p j (c i) -> p c j i", i=4))
 
-        def quantise_w2(b, e, e1):
-            if e == 0:
-                over = "w2_rounded0_4" if b == 1 else None
-                w2_codes[b] = (held([P, E * P], U32, f"w2_words{b}", over), held([P, E * P], U8, f"w2_scales{b}"))
-            words, scales = w2_codes[b]
-            cols = slice(e * P, e1 * P)
-            nc.vector.quantize_mx(
-                out=words[:, cols].bitcast(FP8X4),
-                scales=scales[:, cols],
-                in_=w2_rounded[b, e][:].rearrange("p e n j -> p (e n j)"),
-            )
-
-        def second_product(b, e):
-            g = e // 2
-            if e % 2 == 0:
-                y_banks[b, g] = psum.tile([P, 2 * C], F32, name="bank_y", tag=BANK[b][g])
-            words, scales = w2_codes[b]
-            cols = slice(e * P, (e + 1) * P)
-            nc.tensor.matmul_mx(
-                out=y_banks[b, g][:, (e % 2) * C : (e % 2 + 1) * C],
-                lhsT=words[:, cols].bitcast(FP8X4),
-                lhsT_scale=scales[:, cols],
-                rhs=h_codes[e][0][:].bitcast(FP8X4),
-                rhs_scale=h_codes[e][1][:],
-                start=True,
-                stop=True,
-            )
-
-        def copy_y(b, g, engine="scalar"):
-            if g == 0:
-                y[b] = held([P, SLOTS], F32, f"y{b}", {0: "staged_w2_3_0", 2: "staged_w2_4_2"}.get(b))
+        def second_product(b, g):
             e0, e1 = GROUPS[g]
-            if engine == "vector":
-                nc.vector.tensor_copy(y[b][:, e0 * C : e1 * C], y_banks[b, g][:, 0 : (e1 - e0) * C])
-            else:
-                nc.scalar.copy(y[b][:, e0 * C : e1 * C], y_banks[b, g][:, 0 : (e1 - e0) * C])
+            if g == 0:
+                w2_codes[b] = (held([P, E * P], U32, f"w2_words{b}"), held([P, E * P], U8, f"w2_scales{b}"))
+            words, scales = w2_codes[b]
+            nc.vector.quantize_mx(
+                out=words[:, e0 * P : e1 * P].bitcast(FP8X4),
+                scales=scales[:, e0 * P : e1 * P],
+                in_=w2_rounded[b, e0][:].rearrange("p e n j -> p (e n j)"),
+            )
+            y_banks[b, g] = psum.tile([P, 2 * C], F32, name="bank_y", tag=Y_BANKS[b][g])
+            for e in range(e0, e1):
+                cols = slice(e * P, (e + 1) * P)
+                nc.tensor.matmul_mx(
+                    out=y_banks[b, g][:, (e - e0) * C : (e - e0 + 1) * C],
+                    lhsT=words[:, cols].bitcast(FP8X4),
+                    lhsT_scale=scales[:, cols],
+                    rhs=h_codes[e][0][:].bitcast(FP8X4),
+                    rhs_scale=h_codes[e][1][:],
+                    start=True,
+                    stop=True,
+                )
+
+        def copy_y(b, g, copy):
+            if g == 0:
+                y[b] = held([P, SLOTS], F32, f"y{b}", ("staged_w2_1_0", "staged_w2_1_4", "staged_w2_2_3")[b])
+            e0, e1 = GROUPS[g]
+            copy(y[b][:, e0 * C : e1 * C], y_banks[b, g][:, 0 : (e1 - e0) * C])
 
         def weighted(b, r, t0, t1, over=None):
             term = held([P, t1 - t0], F32, f"term{b}_{r}_{t0}", over)
-            entries = slice(t0 // LIST, t1 // LIST)
-            nc.vector.tensor_tensor(term[:], y[b][:].indirect((pos1_t, pos2_t)[r][:, entries]), gates[r][:, t0:t1], ALU.mult)
+            entries = (pos1_t, pos2_t)[r][:, t0 // LIST : t1 // LIST]
+            nc.vector.tensor_tensor(term[:], y[b][:].indirect(entries), gates[r][:, t0:t1], ALU.mult)
             return term
 
-        def add_on_vector(b, first, second, t0, t1, over=None):
-            total = held([P, t1 - t0], F32, f"total{b}_{t0}", over)
+        def add_on_vector(b, first, second, t0, t1):
+            total = held([P, t1 - t0], F32, f"total{b}_{t0}")
             nc.vector.tensor_tensor(total[:], first, second, ALU.add)
             nc.sync.dma_start(out=out[b * P : (b + 1) * P, t0:t1], in_=total[:])
 
@@ -295,50 +284,48 @@ def tile_moe_pkd_glu_relu_kernel(
                 nc.scalar.copy(total[:, c0 * P : c1 * P], bank[:].rearrange("p c n -> p (c n)"))
             nc.scalar.dma_start(out=out[b * P : (b + 1) * P, :], in_=total[:])
 
-        def qm(b, g):
-            e0, e1 = SPANS[b][g]
-            quantise_w2(b, e0, e1)
-            for e in range(e0, e1):
-                second_product(b, e)
-
-        round_w2(0, 0, "vector")
+        round_w2(0, 0, on_vector)
+        round_w2(0, 1, on_vector)
         hidden(LAST, 0)
+        second_product(0, 0)
         hidden(LAST, 1)
-        round_w2(0, 1, "vector")
+        for e in range(2, E):
+            round_w2(0, e, on_scalar)
+        second_product(0, 1)
         quantise_hidden(LAST)
-        qm(0, 0)
-        for e in range(E):
-            round_w2(1, e, "scalar")
-        round_w2(0, 2, "vector")
-        round_w2(0, 3, "vector")
-        qm(0, 1)
-        round_w2(0, 4, "vector")
-        qm(0, 2)
-        qm(1, 0)
-        qm(1, 1)
-        copy_y(0, 0)
-        copy_y(0, 1)
-        copy_y(0, 2, "vector")
+        second_product(0, 2)
+        round_w2(1, 0, on_scalar)
+        copy_y(0, 0, on_vector)
+        copy_y(0, 1, on_scalar)
+        copy_y(0, 2, on_vector)
+
+        for e in range(1, E):
+            round_w2(1, e, on_scalar)
         first0 = weighted(0, 0, 0, T)
-        copy_y(1, 0)
-        copy_y(1, 1)
-        copy_y(1, 2)
-        second0 = weighted(0, 1, 0, T)
-        for e in range(E):
-            round_w2(2, e, "scalar")
+        for g in range(len(GROUPS)):
+            second_product(1, g)
+        for g in range(len(GROUPS)):
+            copy_y(1, g, on_scalar)
+        second0 = weighted(0, 1, 0, T, over=f"w2_rounded1_{LAST}")
+
+        for e in range(LAST):
+            round_w2(2, e, on_scalar)
         first1 = weighted(1, 0, 0, T)
-        qm(2, 0)
-        qm(2, 1)
-        qm(2, 2)
-        second1 = weighted(1, 1, 0, T, "w2_rounded2_4")
-        for g in range(3):
-            copy_y(2, g)
+        second_product(2, 0)
+        second_product(2, 1)
+        round_w2(2, LAST, on_vector)
+        second_product(2, 2)
+        second1 = weighted(1, 1, 0, T, over=f"w2_rounded2_{LAST}")
+        for g in range(len(GROUPS)):
+            copy_y(2, g, on_scalar)
+
         add_by_transposes(0, first0, second0)
         add_on_vector(1, first1[:], second1[:], 0, T)
         first2 = weighted(2, 0, 0, T)
-        cuts = (0, 320, 512, T)
-        second2 = [weighted(2, 1, cuts[0], cuts[1]), weighted(2, 1, cuts[1], cuts[2])]
-        add_on_vector(2, first2[:, cuts[0] : cuts[1]], second2[0][:], cuts[0], cuts[1])
-        second2.append(weighted(2, 1, cuts[2], cuts[3]))
-        add_on_vector(2, first2[:, cuts[1] : cuts[2]], second2[1][:], cuts[1], cuts[2])
-        add_on_vector(2, first2[:, cuts[2] : cuts[3]], second2[2][:], cuts[2], cuts[3])
+        waiting = None
+        for t0, t1 in zip(LAST_CUTS, LAST_CUTS[1:]):
+            second2 = weighted(2, 1, t0, t1)
+            if waiting is not None:
+                add_on_vector(*waiting)
+            waiting = (2, first2[:, t0:t1], second2[:], t0, t1)
+        add_on_vector(*waiting)

@@ -16,6 +16,7 @@ U16 = mybir.dt.uint16
 U8 = mybir.dt.uint8
 FP8X4 = mybir.dt.float8_e4m3fn_x4
 ALU = mybir.AluOpType
+COPY = mybir.ActivationFunctionType.Copy
 
 P = 128
 PACK = 4
@@ -28,7 +29,7 @@ GROUPS = ((0, 2), (2, 4), (4, 5))
 SCALAR_W3 = 64
 SCALAR_W1 = 88
 SCALAR_W1_LAST = 48
-LAST_CUTS = (0, 320, 512, T)
+LAST_CUTS = (0, 416, T)
 Y_BANKS = (("w3_1_0", "w3_1_1", "w1_1_0"), ("w1_1_1", "w3_0_0", "w3_0_1"), ("w3_1_0", "w3_1_1", "w1_1_0"))
 
 
@@ -245,7 +246,7 @@ def tile_moe_pkd_glu_relu_kernel(
 
         def copy_y(b, g, copy):
             if g == 0:
-                y[b] = held([P, SLOTS], F32, f"y{b}", ("staged_w2_1_0", "staged_w2_1_4", "staged_w2_2_3")[b])
+                y[b] = held([P, SLOTS], F32, f"y{b}", ("staged_w2_1_0", "staged_w2_1_4", "w2_rounded2_2")[b])
             e0, e1 = GROUPS[g]
             copy(y[b][:, e0 * C : e1 * C], y_banks[b, g][:, 0 : (e1 - e0) * C])
 
@@ -255,14 +256,14 @@ def tile_moe_pkd_glu_relu_kernel(
             nc.vector.tensor_tensor(term[:], y[b][:].indirect(entries), gates[r][:, t0:t1], ALU.mult)
             return term
 
-        def add_on_vector(b, first, second, t0, t1):
-            total = held([P, t1 - t0], F32, f"total{b}_{t0}")
+        def add_on_vector(b, first, second, t0, t1, over=None):
+            total = held([P, t1 - t0], F32, f"total{b}_{t0}", over)
             nc.vector.tensor_tensor(total[:], first, second, ALU.add)
             nc.sync.dma_start(out=out[b * P : (b + 1) * P, t0:t1], in_=total[:])
 
         def add_by_transposes(b, first, second):
             total = held([P, T], F32, f"total{b}_0")
-            turned = held([P, T], F32, "turned", "w2_words2")
+            turned = held([P, T], F32, "turned", "staged_w2_2_3")
             runs = ((0, 3), (3, T // P))
             for s, (c0, c1) in enumerate(runs):
                 bank = psum.tile([P, c1 - c0, P], F32, name="bank_turned", tag=f"w1_0_{s}")
@@ -278,7 +279,7 @@ def tile_moe_pkd_glu_relu_kernel(
                         )
                 nc.scalar.copy(turned[:, c0 * P : c1 * P], bank[:].rearrange("p c n -> p (c n)"))
             for s, (c0, c1) in enumerate(runs):
-                bank = psum.tile([P, c1 - c0, P], F32, name="bank_back", tag=("w1_1_1", "w3_0_0")[s])
+                bank = psum.tile([P, c1 - c0, P], F32, name="bank_back", tag=("w1_1_0", "w3_1_1")[s])
                 for c in range(c0, c1):
                     nc.tensor.transpose(bank[:, c - c0, :], turned[:, c * P : (c + 1) * P], ident[:])
                 nc.scalar.copy(total[:, c0 * P : c1 * P], bank[:].rearrange("p c n -> p (c n)"))
@@ -319,13 +320,18 @@ def tile_moe_pkd_glu_relu_kernel(
         for g in range(len(GROUPS)):
             copy_y(2, g, on_scalar)
 
-        add_by_transposes(0, first0, second0)
-        add_on_vector(1, first1[:], second1[:], 0, T)
+        pieces = tuple(zip(LAST_CUTS, LAST_CUTS[1:]))
+        fetched = {}
+        for t0, t1 in pieces:
+            fetched[t0] = held([P, t1 - t0], F32, f"fetched{t0}")
+            nc.scalar.activation(fetched[t0][:], y[2][:].indirect(pos2_t[:, t0 // LIST : t1 // LIST]), COPY)
+            if t0 == 0:
+                add_by_transposes(0, first0, second0)
         first2 = weighted(2, 0, 0, T)
-        waiting = None
-        for t0, t1 in zip(LAST_CUTS, LAST_CUTS[1:]):
-            second2 = weighted(2, 1, t0, t1)
-            if waiting is not None:
-                add_on_vector(*waiting)
-            waiting = (2, first2[:, t0:t1], second2[:], t0, t1)
-        add_on_vector(*waiting)
+        add_on_vector(1, first1[:], second1[:], 0, T, over="gate0")
+        second2 = {}
+        for t0, t1 in pieces:
+            second2[t0] = held([P, t1 - t0], F32, f"term2_1_{t0}")
+            nc.vector.tensor_tensor(second2[t0][:], fetched[t0][:], gates[1][:, t0:t1], ALU.mult)
+        for t0, t1 in pieces:
+            add_on_vector(2, first2[:, t0:t1], second2[t0][:], t0, t1)

@@ -26,6 +26,7 @@ BLOCKS = N // P
 LAST = E - 1
 WINDOW = 704
 GROUPS = ((0, 2), (2, 4), (4, 5))
+SCALAR_FIRST = 72
 SCALAR_W3 = 64
 SCALAR_W1 = 88
 SCALAR_W1_LAST = 48
@@ -40,6 +41,7 @@ def tile_moe_pkd_glu_relu_kernel(
     with ExitStack() as ctx:
         keep = ctx.enter_context(tc.tile_pool(name="keep", bufs=1))
         ring = ctx.enter_context(tc.tile_pool(name="ring", bufs=2))
+        front = ctx.enter_context(tc.tile_pool(name="front", bufs=1))
         psum = ctx.enter_context(tc.psum_pool(name="psum", bufs=1))
 
         def held(shape, dtype, name, over=None):
@@ -62,17 +64,16 @@ def tile_moe_pkd_glu_relu_kernel(
         for e in range(E):
             for label, w in (("w3", w3), ("w1", w1)):
                 rows = w[e].rearrange("(p j) i -> p j i", j=PACK)
-                if (label, e) != ("w3", 0):
+                if (label, e) == ("w3", 0):
+                    staged[label, e] = front.tile([P, PACK, H], F32, name="staged_first", align_bytes=64, offset=0)
+                else:
                     staged[label, e] = held([P, PACK, H], F32, f"staged_{label}_{e}")
-                    nc.sync.dma_start(out=staged[label, e][:], in_=rows)
-                    continue
-                first_halves = [held([P, PACK, H // 2], F32, f"staged_w3_0_{q}") for q in range(2)]
-                nc.sync.dma_start(out=first_halves[0][:], in_=rows[:, :, 0 : H // 2])
-                for r in range(4):
-                    nc.sync.dma_start(
-                        out=token_scales[r:P:32, 0:T].bitcast(I32), in_=x_scales[0, r:16:4, :].bitcast(I32)
-                    )
-                nc.sync.dma_start(out=first_halves[1][:], in_=rows[:, :, H // 2 : H])
+                nc.sync.dma_start(out=staged[label, e][:], in_=rows)
+                if (label, e) == ("w3", 0):
+                    for r in range(4):
+                        nc.sync.dma_start(
+                            out=token_scales[r:P:32, 0:T].bitcast(I32), in_=x_scales[0, r:16:4, :].bitcast(I32)
+                        )
 
         def load_w2(b, e):
             staged["w2", b, e] = held([P, PACK, P], F32, f"staged_w2_{b}_{e}")
@@ -95,7 +96,10 @@ def tile_moe_pkd_glu_relu_kernel(
         slot_words, slot_scales = {}, {}
 
         def gather(window, dtype, into, label, e0, e1, over=None):
-            tile = held([P, (e1 - e0) * C], dtype, f"slot_{label}{e0}", over)
+            if over is None:
+                tile = held([P, (e1 - e0) * C], dtype, f"slot_{label}{e0}")
+            else:
+                tile = front.tile([P, (e1 - e0) * C], dtype, name=f"slot_{label}{e0}", align_bytes=64, offset=over)
             nc.vector.tensor_copy(tile[:], window.indirect(offs_t[:, e0 * C // LIST : e1 * C // LIST]))
             for e in range(e0, e1):
                 into[e] = tile[:, (e - e0) * C : (e - e0 + 1) * C]
@@ -108,20 +112,20 @@ def tile_moe_pkd_glu_relu_kernel(
 
         rounded, codes, banks, up, h_rounded, h_codes = {}, {}, {}, {}, {}, {}
 
+        def on_gpsimd(target, source):
+            nc.gpsimd.tensor_scalar(target, source, 1.0, 0.0, ALU.mult, ALU.add)
+
         def product_steps(label, e):
             return (slice(2, 4), slice(0, 2)) if (label, e) == ("w1", LAST) else (slice(0, PACK),)
 
         def round_first(label, e):
             rounded[label, e] = ring.tile([P, PACK, P, PACK], BF16, name=f"rounded_{label}", align_bytes=64)
             target = rounded[label, e][:].rearrange("p t m j -> p m j t")
-            if (label, e) == ("w3", 0):
-                for q, half in enumerate(first_halves):
-                    source = half[:].rearrange("p j (m t) -> p m j t", t=PACK)
-                    nc.scalar.copy(target[:, q * P // 2 : (q + 1) * P // 2], source)
-                return
             source = staged[label, e][:].rearrange("p j (m t) -> p m j t", t=PACK)
             if e == 0:
-                nc.scalar.copy(target, source)
+                nc.scalar.copy(target[:, 0:SCALAR_FIRST], source[:, 0:SCALAR_FIRST])
+                order = "p m j t -> p m t j"
+                on_gpsimd(target[:, SCALAR_FIRST:P].rearrange(order), source[:, SCALAR_FIRST:P].rearrange(order))
                 return
             if label == "w3":
                 cut = SCALAR_W3
@@ -208,8 +212,8 @@ def tile_moe_pkd_glu_relu_kernel(
                 quantise_hidden(e - 1)
             first_product("w1", e)
             if e == 0:
-                gather_words(LAST, E, over="staged_w3_0_0")
-                gather_scales(LAST, E, over="staged_w3_0_1")
+                gather_words(LAST, E, over=0)
+                gather_scales(LAST, E, over=4 * C)
 
         w2_rounded, w2_codes, y, y_banks = {}, {}, {}, {}
         on_vector, on_scalar = nc.vector.tensor_copy, nc.scalar.copy

@@ -26,9 +26,10 @@ BLOCKS = N // P
 LAST = E - 1
 WINDOW = 704
 GROUPS = ((0, 2), (2, 4), (4, 5))
-SCALAR_FIRST = 72
-SCALAR_W3 = 64
-SCALAR_W1 = 88
+SCALAR_FIRST = 80
+SCALAR_W3 = 45
+VECTOR_W3 = 39
+SCALAR_W1 = 104
 SCALAR_W1_LAST = 48
 LAST_CUTS = (0, 416, T)
 Y_BANKS = (("w3_1_0", "w3_1_1", "w1_1_0"), ("w1_1_1", "w3_0_0", "w3_0_1"), ("w3_1_0", "w3_1_1", "w1_1_0"))
@@ -119,7 +120,10 @@ def tile_moe_pkd_glu_relu_kernel(
             return (slice(2, 4), slice(0, 2)) if (label, e) == ("w1", LAST) else (slice(0, PACK),)
 
         def round_first(label, e):
-            rounded[label, e] = ring.tile([P, PACK, P, PACK], BF16, name=f"rounded_{label}", align_bytes=64)
+            slot = e if label == "w1" else e - 1 if e >= 1 else E
+            rounded[label, e] = front.tile(
+                [P, PACK, P, PACK], BF16, name=f"rounded_{label}_{e}", align_bytes=64, offset=8192 + slot * 4096
+            )
             target = rounded[label, e][:].rearrange("p t m j -> p m j t")
             source = staged[label, e][:].rearrange("p j (m t) -> p m j t", t=PACK)
             if e == 0:
@@ -128,9 +132,13 @@ def tile_moe_pkd_glu_relu_kernel(
                 on_gpsimd(target[:, SCALAR_FIRST:P].rearrange(order), source[:, SCALAR_FIRST:P].rearrange(order))
                 return
             if label == "w3":
-                cut = SCALAR_W3
-            else:
-                cut = SCALAR_W1_LAST if e == LAST else SCALAR_W1
+                cut = SCALAR_W3 + VECTOR_W3
+                nc.scalar.copy(target[:, 0:SCALAR_W3], source[:, 0:SCALAR_W3])
+                nc.vector.tensor_copy(target[:, SCALAR_W3:cut], source[:, SCALAR_W3:cut])
+                order = "p m j t -> p m t j"
+                on_gpsimd(target[:, cut:P].rearrange(order), source[:, cut:P].rearrange(order))
+                return
+            cut = SCALAR_W1_LAST if e == LAST else SCALAR_W1
             for ts in product_steps(label, e):
                 nc.scalar.copy(target[:, 0:cut, :, ts], source[:, 0:cut, :, ts])
             for ts in product_steps(label, e):

@@ -27,6 +27,8 @@ LAST = E - 1
 WINDOW = 704
 GROUPS = ((0, 2), (2, 4), (4, 5))
 SCALAR_FIRST = 80
+SCALAR_FIRST_W1 = 88
+FIRST_W3_AT = ((PACK - 1) * P + SCALAR_FIRST_W1) * PACK
 SCALAR_W3 = 45
 VECTOR_W3 = 39
 SCALAR_W1 = 104
@@ -113,6 +115,8 @@ def tile_moe_pkd_glu_relu_kernel(
 
         rounded, codes, banks, up, h_rounded, h_codes = {}, {}, {}, {}, {}, {}
 
+        first_rounded = front.tile([P, FIRST_W3_AT + PACK * H], BF16, name="first_rounded", align_bytes=64, offset=8192)
+
         def on_gpsimd(target, source):
             nc.gpsimd.tensor_scalar(target, source, 1.0, 0.0, ALU.mult, ALU.add)
 
@@ -120,16 +124,22 @@ def tile_moe_pkd_glu_relu_kernel(
             return (slice(2, 4), slice(0, 2)) if (label, e) == ("w1", LAST) else (slice(0, PACK),)
 
         def round_first(label, e):
-            slot = e if label == "w1" else e - 1 if e >= 1 else E
-            rounded[label, e] = front.tile(
-                [P, PACK, P, PACK], BF16, name=f"rounded_{label}_{e}", align_bytes=64, offset=8192 + slot * 4096
-            )
-            target = rounded[label, e][:].rearrange("p t m j -> p m j t")
+            if e == 0:
+                start = FIRST_W3_AT if label == "w3" else 0
+                run = first_rounded[:, start : start + PACK * H]
+                rounded[label, e] = run.rearrange("p (t m j) -> p t m j", t=PACK, j=PACK)
+            else:
+                slot = e if label == "w1" else e - 1
+                rounded[label, e] = front.tile(
+                    [P, PACK, P, PACK], BF16, name=f"rounded_{label}_{e}", align_bytes=64, offset=8192 + slot * 4096
+                )[:]
+            target = rounded[label, e].rearrange("p t m j -> p m j t")
             source = staged[label, e][:].rearrange("p j (m t) -> p m j t", t=PACK)
             if e == 0:
-                nc.scalar.copy(target[:, 0:SCALAR_FIRST], source[:, 0:SCALAR_FIRST])
+                cut = SCALAR_FIRST if label == "w3" else SCALAR_FIRST_W1
+                nc.scalar.copy(target[:, 0:cut], source[:, 0:cut])
                 order = "p m j t -> p m t j"
-                on_gpsimd(target[:, SCALAR_FIRST:P].rearrange(order), source[:, SCALAR_FIRST:P].rearrange(order))
+                on_gpsimd(target[:, cut:P].rearrange(order), source[:, cut:P].rearrange(order))
                 return
             if label == "w3":
                 cut = SCALAR_W3 + VECTOR_W3

from contextlib import ExitStack

import concourse.mybir as mybir
from concourse.masks import make_identity

K, T, E, C, H, N = 512, 640, 5, 256, 512, 384
SLOTS = E * C
FLOPS = 2 * SLOTS * (2 * K * H + H * N)
BYTES = 4 * E * (2 * K * H + H * N) + K * T + (K // 32) * T + 4 * 2 * T + 2 * (SLOTS + 2 * T) + 4 * N * T

F32 = mybir.dt.float32
BF16 = mybir.dt.bfloat16
I32 = mybir.dt.int32
U32 = mybir.dt.uint32
U16 = mybir.dt.uint16
U8 = mybir.dt.uint8
FP8X4 = mybir.dt.float8_e4m3fn_x4
ALU = mybir.AluOpType
COPY = mybir.ActivationFunctionType.Copy

P = 128
PACK = 4
LIST = 16
HALF = C // 2
BLOCKS = N // P
LAST = E - 1
WINDOW = 704
GROUPS = ((0, 2), (2, 4), (4, 5))
SCALAR_FIRST = 80
SCALAR_FIRST_W1 = 88
FIRST_W3_AT = ((PACK - 1) * P + SCALAR_FIRST_W1) * PACK
SCALAR_W3 = 45
VECTOR_W3 = 39
SCALAR_W1 = 104
SCALAR_W1_LAST = 48
LAST_CUTS = (0, 416, T)
Y_BANKS = (("w3_1_0", "w3_1_1", "w1_1_0"), ("w1_1_1", "w3_0_0", "w3_0_1"), ("w3_1_0", "w3_1_1", "w1_1_0"))


def tile_moe_pkd_glu_relu_kernel(
    tc, x_words, x_scales, w1, w3, w2, gate, offs, pos1, pos2, out
):
    nc = tc.nc
    with ExitStack() as ctx:
        keep = ctx.enter_context(tc.tile_pool(name="keep", bufs=1))
        ring = ctx.enter_context(tc.tile_pool(name="ring", bufs=2))
        front = ctx.enter_context(tc.tile_pool(name="front", bufs=1))
        psum = ctx.enter_context(tc.psum_pool(name="psum", bufs=1))

        def held(shape, dtype, name, over=None):
            return keep.tile(shape, dtype, name=name, tag=over or name, align_bytes=64)

        token_words = held([P, WINDOW], I32, "token_words")
        token_scales = held([P, WINDOW], U8, "token_scales")
        offs_t = keep.tile([P, SLOTS // LIST], U16, name="offs_t")
        pos1_t = keep.tile([P, T // LIST], U16, name="pos1_t")
        pos2_t = keep.tile([P, T // LIST], U16, name="pos2_t")
        gates = [held([P, T], F32, f"gate{r}") for r in range(2)]
        ident = held([P, P], F32, "ident")
        nc.gpsimd.memset(token_scales[:].bitcast(I32), 0)
        nc.gpsimd.memset(token_words[:, T:WINDOW], 0)
        make_identity(nc, ident[:])
        nc.sync.dma_start(out=token_words[:, 0:T], in_=x_words[0].rearrange("p t r -> p (t r)").bitcast(I32))
        nc.sync.dma_start(out=offs_t[:], in_=offs)

        staged = {}
        for e in range(E):
            for label, w in (("w3", w3), ("w1", w1)):
                rows = w[e].rearrange("(p j) i -> p j i", j=PACK)
                if (label, e) == ("w3", 0):
                    staged[label, e] = front.tile([P, PACK, H], F32, name="staged_first", align_bytes=64, offset=0)
                else:
                    staged[label, e] = held([P, PACK, H], F32, f"staged_{label}_{e}")
                nc.sync.dma_start(out=staged[label, e][:], in_=rows)
                if (label, e) == ("w3", 0):
                    for r in range(4):
                        nc.sync.dma_start(
                            out=token_scales[r:P:32, 0:T].bitcast(I32), in_=x_scales[0, r:16:4, :].bitcast(I32)
                        )

        def load_w2(b, e):
            staged["w2", b, e] = held([P, PACK, P], F32, f"staged_w2_{b}_{e}")
            nc.sync.dma_start(
                out=staged["w2", b, e][:], in_=w2[e, :, b * P : (b + 1) * P].rearrange("(p j) n -> p j n", j=PACK)
            )

        def load_gate(r):
            nc.sync.dma_start(out=(pos1_t, pos2_t)[r][:], in_=(pos1, pos2)[r])
            nc.sync.dma_start(out=gates[r][:], in_=gate[r, 0:P, :])

        for b in range(BLOCKS):
            for e in range(E):
                load_w2(b, e)
                if (b, e) == (1, 1):
                    load_gate(0)
            if b == 1:
                load_gate(1)

        slot_words, slot_scales = {}, {}

        def gather(window, dtype, into, label, e0, e1, over=None):
            if over is None:
                tile = held([P, (e1 - e0) * C], dtype, f"slot_{label}{e0}")
            else:
                tile = front.tile([P, (e1 - e0) * C], dtype, name=f"slot_{label}{e0}", align_bytes=64, offset=over)
            nc.vector.tensor_copy(tile[:], window.indirect(offs_t[:, e0 * C // LIST : e1 * C // LIST]))
            for e in range(e0, e1):
                into[e] = tile[:, (e - e0) * C : (e - e0 + 1) * C]

        def gather_words(e0, e1, over=None):
            gather(token_words[:].bitcast(U32), U32, slot_words, "words", e0, e1, over)

        def gather_scales(e0, e1, over=None):
            gather(token_scales[:], U8, slot_scales, "scales", e0, e1, over)

        rounded, codes, banks, up, h_rounded, h_codes = {}, {}, {}, {}, {}, {}

        first_rounded = front.tile([P, FIRST_W3_AT + PACK * H], BF16, name="first_rounded", align_bytes=64, offset=8192)

        def on_gpsimd(target, source):
            nc.gpsimd.tensor_scalar(target, source, 1.0, 0.0, ALU.mult, ALU.add)

        def product_steps(label, e):
            return (slice(2, 4), slice(0, 2)) if (label, e) == ("w1", LAST) else (slice(0, PACK),)

        def round_first(label, e):
            if e == 0:
                start = FIRST_W3_AT if label == "w3" else 0
                run = first_rounded[:, start : start + PACK * H]
                rounded[label, e] = run.rearrange("p (t m j) -> p t m j", t=PACK, j=PACK)
            else:
                slot = e if label == "w1" else e - 1
                rounded[label, e] = front.tile(
                    [P, PACK, P, PACK], BF16, name=f"rounded_{label}_{e}", align_bytes=64, offset=8192 + slot * 4096
                )[:]
            target = rounded[label, e].rearrange("p t m j -> p m j t")
            source = staged[label, e][:].rearrange("p j (m t) -> p m j t", t=PACK)
            if e == 0:
                cut = SCALAR_FIRST if label == "w3" else SCALAR_FIRST_W1
                nc.scalar.copy(target[:, 0:cut], source[:, 0:cut])
                order = "p m j t -> p m t j"
                on_gpsimd(target[:, cut:P].rearrange(order), source[:, cut:P].rearrange(order))
                return
            if label == "w3":
                cut = SCALAR_W3 + VECTOR_W3
                nc.scalar.copy(target[:, 0:SCALAR_W3], source[:, 0:SCALAR_W3])
                nc.vector.tensor_copy(target[:, SCALAR_W3:cut], source[:, SCALAR_W3:cut])
                order = "p m j t -> p m t j"
                on_gpsimd(target[:, cut:P].rearrange(order), source[:, cut:P].rearrange(order))
                return
            cut = SCALAR_W1_LAST if e == LAST else SCALAR_W1
            for ts in product_steps(label, e):
                nc.scalar.copy(target[:, 0:cut, :, ts], source[:, 0:cut, :, ts])
            for ts in product_steps(label, e):
                nc.vector.tensor_copy(target[:, cut:P, :, ts], source[:, cut:P, :, ts])

        def quantise_first(label, e):
            words = ring.tile([P, H], U32, name=f"words_{label}", align_bytes=64)
            scales = ring.tile([P, H], U8, name=f"scales_{label}", align_bytes=64)
            for ts in product_steps(label, e):
                cols = slice(ts.start * P, ts.stop * P)
                nc.vector.quantize_mx(
                    out=words[:, cols].bitcast(FP8X4),
                    scales=scales[:, cols],
                    in_=rounded[label, e][:, ts].rearrange("p t m j -> p (t m j)"),
                )
            codes[label, e] = (words, scales)

        def first_product(label, e):
            for s in range(2):
                banks[label, e, s] = psum.tile([P, PACK, HALF], F32, name=f"bank_{label}", tag=f"{label}_{e % 2}_{s}")
            words, scales = codes[label, e]
            for ts in product_steps(label, e):
                for s in range(2):
                    slots = slice(s * HALF, (s + 1) * HALF)
                    for t in range(ts.start, ts.stop):
                        cols = slice(t * P, (t + 1) * P)
                        nc.tensor.matmul_mx(
                            out=banks[label, e, s][:, t, :],
                            lhsT=words[:, cols].bitcast(FP8X4),
                            lhsT_scale=scales[:, cols],
                            rhs=slot_words[e][:, slots].bitcast(FP8X4),
                            rhs_scale=slot_scales[e][:, slots],
                            start=True,
                            stop=True,
                        )

        def copy_up(e):
            host = staged["w1", e]
            for s in range(2):
                up[e, s] = host[:, :, s * P : (s + 1) * P].rearrange("p r (c t) -> p r c t", t=PACK)
                nc.scalar.copy(up[e, s], banks["w3", e, s][:].rearrange("p t (r c) -> p r c t", r=PACK))

        def hidden(e, s):
            if s == 0:
                h_rounded[e] = held([P, 2, HALF, PACK], BF16, f"h_rounded{e}")
            nc.vector.scalar_tensor_tensor(
                out=h_rounded[e][:, s].rearrange("p (r c) t -> p r c t", r=PACK),
                in0=banks["w1", e, s][:].rearrange("p t (r c) -> p r c t", r=PACK),
                scalar=0.0,
                in1=up[e, s],
                op0=ALU.max,
                op1=ALU.mult,
            )

        def quantise_hidden(e):
            words = held([P, C], U32, f"h_words{e}")
            scales = held([P, C], U8, f"h_scales{e}")
            nc.vector.quantize_mx(
                out=words[:].bitcast(FP8X4), scales=scales[:], in_=h_rounded[e][:].rearrange("p s c t -> p (s c t)")
            )
            h_codes[e] = (words, scales)

        for e0, e1 in GROUPS[:-1]:
            gather_words(e0, e1)
        for e0, e1 in GROUPS[:-1]:
            gather_scales(e0, e1)
        for e in range(E):
            round_first("w3", e)
            quantise_first("w3", e)
            if e >= 1:
                hidden(e - 1, 0)
            first_product("w3", e)
            round_first("w1", e)
            if e >= 1:
                hidden(e - 1, 1)
            copy_up(e)
            quantise_first("w1", e)
            if e >= 1:
                quantise_hidden(e - 1)
            first_product("w1", e)
            if e == 0:
                gather_words(LAST, E, over=0)
                gather_scales(LAST, E, over=4 * C)

        w2_rounded, w2_codes, y, y_banks = {}, {}, {}, {}
        on_vector, on_scalar = nc.vector.tensor_copy, nc.scalar.copy

        def round_w2(b, e, copy):
            e0, e1 = GROUPS[e // 2]
            if e == e0:
                w2_rounded[b, e0] = held([P, e1 - e0, P, PACK], BF16, f"w2_rounded{b}_{e0}")
            target = w2_rounded[b, e0][:, e - e0].rearrange("p (c i) j -> p c j i", i=4)
            copy(target, staged["w2", b, e][:].rearrange("p j (c i) -> p c j i", i=4))

        def second_product(b, g):
            e0, e1 = GROUPS[g]
            if g == 0:
                w2_codes[b] = (held([P, E * P], U32, f"w2_words{b}"), held([P, E * P], U8, f"w2_scales{b}"))
            words, scales = w2_codes[b]
            nc.vector.quantize_mx(
                out=words[:, e0 * P : e1 * P].bitcast(FP8X4),
                scales=scales[:, e0 * P : e1 * P],
                in_=w2_rounded[b, e0][:].rearrange("p e n j -> p (e n j)"),
            )
            y_banks[b, g] = psum.tile([P, 2 * C], F32, name="bank_y", tag=Y_BANKS[b][g])
            for e in range(e0, e1):
                cols = slice(e * P, (e + 1) * P)
                nc.tensor.matmul_mx(
                    out=y_banks[b, g][:, (e - e0) * C : (e - e0 + 1) * C],
                    lhsT=words[:, cols].bitcast(FP8X4),
                    lhsT_scale=scales[:, cols],
                    rhs=h_codes[e][0][:].bitcast(FP8X4),
                    rhs_scale=h_codes[e][1][:],
                    start=True,
                    stop=True,
                )

        def copy_y(b, g, copy):
            if g == 0:
                y[b] = held([P, SLOTS], F32, f"y{b}", ("staged_w2_1_0", "staged_w2_1_4", "w2_rounded2_2")[b])
            e0, e1 = GROUPS[g]
            copy(y[b][:, e0 * C : e1 * C], y_banks[b, g][:, 0 : (e1 - e0) * C])

        def weighted(b, r, t0, t1, over=None):
            term = held([P, t1 - t0], F32, f"term{b}_{r}_{t0}", over)
            entries = (pos1_t, pos2_t)[r][:, t0 // LIST : t1 // LIST]
            nc.vector.tensor_tensor(term[:], y[b][:].indirect(entries), gates[r][:, t0:t1], ALU.mult)
            return term

        def add_on_vector(b, first, second, t0, t1, over=None):
            total = held([P, t1 - t0], F32, f"total{b}_{t0}", over)
            nc.vector.tensor_tensor(total[:], first, second, ALU.add)
            nc.sync.dma_start(out=out[b * P : (b + 1) * P, t0:t1], in_=total[:])

        def add_by_transposes(b, first, second):
            total = held([P, T], F32, f"total{b}_0")
            turned = held([P, T], F32, "turned", "staged_w2_2_3")
            runs = ((0, 3), (3, T // P))
            for s, (c0, c1) in enumerate(runs):
                bank = psum.tile([P, c1 - c0, P], F32, name="bank_turned", tag=f"w1_0_{s}")
                for c in range(c0, c1):
                    for term in (first, second):
                        nc.tensor.matmul(
                            bank[:, c - c0, :],
                            term[:, c * P : (c + 1) * P],
                            ident[:],
                            is_transpose=True,
                            start=term is first,
                            stop=term is second,
                        )
                nc.scalar.copy(turned[:, c0 * P : c1 * P], bank[:].rearrange("p c n -> p (c n)"))
            for s, (c0, c1) in enumerate(runs):
                bank = psum.tile([P, c1 - c0, P], F32, name="bank_back", tag=("w1_1_0", "w3_1_1")[s])
                for c in range(c0, c1):
                    nc.tensor.transpose(bank[:, c - c0, :], turned[:, c * P : (c + 1) * P], ident[:])
                nc.scalar.copy(total[:, c0 * P : c1 * P], bank[:].rearrange("p c n -> p (c n)"))
            nc.scalar.dma_start(out=out[b * P : (b + 1) * P, :], in_=total[:])

        round_w2(0, 0, on_vector)
        round_w2(0, 1, on_vector)
        hidden(LAST, 0)
        second_product(0, 0)
        hidden(LAST, 1)
        for e in range(2, E):
            round_w2(0, e, on_scalar)
        second_product(0, 1)
        quantise_hidden(LAST)
        second_product(0, 2)
        round_w2(1, 0, on_scalar)
        copy_y(0, 0, on_vector)
        copy_y(0, 1, on_scalar)
        copy_y(0, 2, on_vector)

        for e in range(1, E):
            round_w2(1, e, on_scalar)
        first0 = weighted(0, 0, 0, T)
        for g in range(len(GROUPS)):
            second_product(1, g)
        for g in range(len(GROUPS)):
            copy_y(1, g, on_scalar)
        second0 = weighted(0, 1, 0, T, over=f"w2_rounded1_{LAST}")

        for e in range(LAST):
            round_w2(2, e, on_scalar)
        first1 = weighted(1, 0, 0, T)
        second_product(2, 0)
        second_product(2, 1)
        round_w2(2, LAST, on_vector)
        second_product(2, 2)
        second1 = weighted(1, 1, 0, T, over=f"w2_rounded2_{LAST}")
        for g in range(len(GROUPS)):
            copy_y(2, g, on_scalar)

        pieces = tuple(zip(LAST_CUTS, LAST_CUTS[1:]))
        fetched = {}
        for t0, t1 in pieces:
            fetched[t0] = held([P, t1 - t0], F32, f"fetched{t0}")
            nc.scalar.activation(fetched[t0][:], y[2][:].indirect(pos2_t[:, t0 // LIST : t1 // LIST]), COPY)
            if t0 == 0:
                add_by_transposes(0, first0, second0)
        first2 = weighted(2, 0, 0, T)
        add_on_vector(1, first1[:], second1[:], 0, T, over="gate0")
        second2 = {}
        for t0, t1 in pieces:
            second2[t0] = held([P, t1 - t0], F32, f"term2_1_{t0}")
            nc.vector.tensor_tensor(second2[t0][:], fetched[t0][:], gates[1][:, t0:t1], ALU.mult)
        for t0, t1 in pieces:
            add_on_vector(2, first2[:, t0:t1], second2[t0][:], t0, t1)
